import numpy as np
import ml_dtypes


def mxq(x, axis, fmt="e4m3"):
    dtype, down = {"e4m3": (ml_dtypes.float8_e4m3fn, 7), "e5m2": (ml_dtypes.float8_e5m2, 14)}[fmt]
    v = np.moveaxis(np.asarray(x, np.float32).astype(ml_dtypes.bfloat16).astype(np.float64), axis, -1)
    blocks = v.reshape(v.shape[:-1] + (-1, 32))
    amax = np.abs(blocks).max(-1, keepdims=True)
    byte = np.maximum(np.where(amax > 0, np.frexp(amax)[1] - 1 + 127, 0) - down, 1)
    scale = np.exp2(byte - 127.0)
    codes = (blocks / scale).astype(np.float32).astype(dtype).astype(np.float64)
    return np.moveaxis((codes * scale).reshape(v.shape), -1, axis)


WIDE = False


def mx_kscale(k):
    if not WIDE:
        return np.ones(k)
    levels = np.array([10, -10, 5, -5, 0])
    if k % 512:
        return np.exp2(np.random.permutation(np.resize(levels, k // 32))).repeat(32)
    a = np.empty((k // 512, 16))
    for p in range(k // 512):
        a[p, :8] = np.random.permutation(np.resize(levels, 8))
        for g in range(8):
            far = levels[np.abs(levels - a[p, g]) >= 10]
            a[p, g + 8] = far[np.random.randint(len(far))]
    return np.exp2(a.ravel()).repeat(32)


BF16 = ml_dtypes.bfloat16


def bf(x):
    return np.asarray(x, np.float32).astype(BF16)


def f64(x):
    return np.asarray(x).astype(np.float64)

def planes(Y):
    n, m = Y.shape
    b = f64(bf(Y)).reshape(n // 32, 32, m)
    amax = np.abs(b).max(1)
    byte = np.clip(np.where(amax > 0, np.frexp(amax)[1] - 1 + 127 - 7, 1), 1, 254)
    codes = (b * np.exp2(127.0 - byte)[:, None, :]).reshape(n, m).astype(np.float32).astype(ml_dtypes.float8_e4m3fn).view(np.uint8)
    words = codes.reshape(n // 512, 128, 4, m).transpose(0, 1, 3, 2)
    return np.ascontiguousarray(words), np.ascontiguousarray(byte.astype(np.uint8).reshape(n // 512, 16, m))


T, N, W = 1024, 2048, 512


def l2_normalize_rows(x, gain):
    length = np.sqrt(np.sum(x * x, axis=-1, keepdims=True) + 1e-6)
    return gain * x / length


def softmax_last(x):
    shifted = x - np.max(x, axis=-1, keepdims=True)
    e = np.exp(shifted)
    return e / np.sum(e, axis=-1, keepdims=True)


def setup_inputs():
    u, t = mx_kscale(W), mx_kscale(T)
    return {
        "key": bf(np.random.standard_normal((T, W)) / u),
        "mem": bf(np.random.standard_normal((N, W))),
        "gm": bf((1.0 + 0.1 * np.random.standard_normal(W)) * u),
        "s": bf(np.random.standard_normal(T) * t),
        "erase": bf((0.5 + 0.5 * np.random.standard_normal((T, W))) / t[:, None]),
        "add": bf(0.7 * np.random.standard_normal((T, W)) / t[:, None]),
    }


def core(key, mem, gm, s, erase, add):
    key, mem, gm, s, erase, add = f64(key), f64(mem), f64(gm), f64(s), f64(erase), f64(add)
    n_tokens = key.shape[0]
    n_rows = mem.shape[0]
    mn = l2_normalize_rows(mem, gm)
    cl = mxq(key, 1, "e4m3") @ mxq(mn, 1, "e4m3").T
    p = softmax_last(cl)
    scale = n_rows / np.sqrt(n_tokens)
    w = (s * scale)[:, None] * p
    wq = mxq(w, 0, "e4m3").T
    er = wq @ mxq(erase, 0, "e4m3")
    ad = wq @ mxq(add, 0, "e4m3")
    return mem * (1.0 - er) + ad


def reference(key, mem, gm, s, erase, add):
    R_out = core(key, mem, gm, s, erase, add)
    words, scales = planes(R_out)
    return R_out, words, scales

@@ -1,0 +1,491 @@
+from contextlib import ExitStack
+
+import concourse.mybir as mybir
+from concourse.masks import make_identity
+
+T, N, W = 1024, 2048, 512
+P, J, G = 128, 4, 512
+TG, NG = T // G, N // G
+FLOPS = 3 * 2 * T * N * W
+
+F32 = mybir.dt.float32
+BF16 = mybir.dt.bfloat16
+U32 = mybir.dt.uint32
+I32 = mybir.dt.int32
+U8 = mybir.dt.uint8
+FP8X4 = mybir.dt.float8_e4m3fn_x4
+ALU = mybir.AluOpType
+ACT = mybir.ActivationFunctionType
+AX = mybir.AxisListType
+
+
+def tile_ntmcontentaddresseraseadd_x1_kernel(tc, key, mem, gm, s, erase, add, out_0, out_1, out_2):
+    nc = tc.nc
+    V, S, GP, PE = nc.vector, nc.scalar, nc.gpsimd, nc.tensor
+    with ExitStack() as ctx:
+        keep = ctx.enter_context(tc.tile_pool(name="keep", bufs=1))
+        work = ctx.enter_context(tc.tile_pool(name="work", bufs=2))
+        psum = ctx.enter_context(tc.psum_pool(name="psum", bufs=1))
+
+        def rows(x, g):
+            return x.rearrange("(g p t) w -> g p t w", p=P, t=J)[g]
+
+        def keep_tile(name, shape, dt):
+            return keep.tile(shape, dt, name=name, tag=name, align_bytes=64)
+
+        def bank(k, name):
+            return psum.tile([P, 512], F32, name=name, tag="b%d" % k)
+
+        mem_sb = [keep_tile("mem%d" % g, [P, J, W], BF16) for g in range(NG)]
+        key_sb = [keep_tile("key%d" % g, [P, J, W], BF16) for g in range(TG)]
+        ea_sb = {}
+        for x in ("er", "ad"):
+            for g in range(TG):
+                ea_sb[x, g] = keep_tile("%s%d" % (x, g), [P, J, W], BF16)
+        gm_row = keep_tile("gm_row", [P, W], BF16)
+        ones = keep_tile("ones", [P, P], BF16)
+        s_sb = keep_tile("s_sb", [P, TG, J], BF16)
+        ident = keep_tile("ident", [P, P], F32)
+        mhalf = keep_tile("mhalf", [P, J], F32)
+        gm_b = keep_tile("gm_b", [P, W], F32)
+        ssq = keep_tile("ssq", [P, NG, J], F32)
+        ssqe = keep_tile("ssqe", [P, NG, J], F32)
+        rinv = keep_tile("rinv", [P, NG, J], F32)
+        mq = keep_tile("mq", [P, NG, G], U32)
+        ms = keep_tile("ms", [P, NG, G], U8)
+        kq = keep_tile("kq", [P, TG, G], U32)
+        ks = keep_tile("ks", [P, TG, G], U8)
+        wq = [keep_tile("wq%d" % g, [P, N], U32) for g in range(TG)]
+        wsc = [keep_tile("wsc%d" % g, [P, N], U8) for g in range(TG)]
+        eq = {}
+        es = {}
+        for x in ("er", "ad"):
+            for g in range(TG):
+                eq[x, g] = keep_tile("q%s%d" % (x, g), [P, W], U32)
+                es[x, g] = keep_tile("s%s%d" % (x, g), [P, W], U8)
+        e_sb = [keep_tile("e%d" % g, [P, J, N], F32) for g in range(TG)]
+        mx = keep_tile("mx", [P, TG * J, NG], F32)
+        nmax = keep_tile("nmax", [P, TG * J], F32)
+        sums = keep_tile("sums", [P, TG * J, NG], F32)
+        tot = keep_tile("tot", [P, TG, J], F32)
+        rtot = keep_tile("rtot", [P, TG, J], F32)
+        coef = keep_tile("coef", [P, TG, J], F32)
+
+        V.memset(gm_row[:], 0.0)
+        V.memset(ones[:], 1.0)
+        GP.dma_start(out=gm_row[0:1, :], in_=gm.rearrange("(o w) -> o w", o=1))
+        GP.dma_start(out=s_sb[:], in_=s.rearrange("(g p t) -> p g t", p=P, t=J))
+        make_identity(nc, ident[:])
+        GP.memset(mhalf[:], -0.5)
+        nc.sync.dma_start(out=mem_sb[0][:, 0:2, :], in_=rows(mem, 0)[:, 0:2, :])
+        nc.sync.dma_start(out=mem_sb[0][:, 2:4, :], in_=rows(mem, 0)[:, 2:4, :])
+        nc.sync.dma_start(out=key_sb[0][:], in_=rows(key, 0))
+        nc.sync.dma_start(out=mem_sb[1][:], in_=rows(mem, 1))
+        nc.sync.dma_start(out=key_sb[1][:], in_=rows(key, 1))
+        nc.sync.dma_start(out=mem_sb[2][:], in_=rows(mem, 2))
+        nc.sync.dma_start(out=mem_sb[3][:], in_=rows(mem, 3))
+        for g in range(TG):
+            nc.sync.dma_start(out=ea_sb["er", g][:], in_=rows(erase, g))
+            nc.sync.dma_start(out=ea_sb["ad", g][:], in_=rows(add, g))
+
+        trb = {}
+
+        def gm_bcast():
+            b = bank(7, "gmps")
+            PE.matmul(b[:], lhsT=ones[:], rhs=gm_row[:], start=True, stop=True)
+            trb["gm"] = b
+
+        def gm_copy():
+            S.copy(gm_b[:], trb["gm"][:])
+
+        def sq(g, ts):
+            for t in ts:
+                junk = work.tile([P, W], BF16, name="junk", tag="junk")
+                S.activation(out=junk[:], in_=mem_sb[g][:, t, :], func=ACT.Square, accum_out=ssq[:, g, t : t + 1])
+
+        def sqv(g, ts):
+            for t in ts:
+                junk = work.tile([P, W], BF16, name="junkv", tag="junkv")
+                V.scalar_tensor_tensor(out=junk[:], in0=mem_sb[g][:, t, :], scalar=1.0, in1=mem_sb[g][:, t, :], op0=ALU.mult, op1=ALU.mult, accum_out=ssq[:, g, t : t + 1])
+
+        def rn(g):
+            GP.tensor_scalar(out=ssqe[:, g, :], in0=ssq[:, g, :], scalar1=1e-6, scalar2=1.0, op0=ALU.add, op1=ALU.mult)
+            GP.tensor_tensor(out=rinv[:, g, :], in0=ssqe[:, g, :], in1=mhalf[:], op=ALU.pow)
+
+        mnr = {}
+
+        def mn(g, ts):
+            for t in ts:
+                m = work.tile([P, W], BF16, name="mnr", tag="mnr", bufs=6)
+                V.scalar_tensor_tensor(out=m[:], in0=mem_sb[g][:, t, :], scalar=rinv[:, g, t : t + 1], in1=trb["gm"][:], op0=ALU.mult, op1=ALU.mult)
+                mnr[g, t] = m
+
+        xg = {}
+
+        def mnx(g, ts):
+            for t in ts:
+                x = work.tile([P, W], F32, name="xg", tag="xg", bufs=4)
+                GP.tensor_tensor(out=x[:], in0=mem_sb[g][:, t, :], in1=gm_b[:], op=ALU.mult)
+                xg[g, t] = x
+
+        def mns(g, ts):
+            for t in ts:
+                m = work.tile([P, W], BF16, name="mnr", tag="mnr", bufs=6)
+                S.activation(out=m[:], in_=xg[g, t][:], func=ACT.Copy, scale=rinv[:, g, t : t + 1])
+                mnr[g, t] = m
+
+        def tr(what, g, h, bk):
+            b = bank(bk, "tr")
+            v = b[:].rearrange("p (i u r) -> p i u r", i=2, u=2)
+            for i in range(2):
+                t = 2 * h + i
+                src = mnr[g, t][:] if what == "m" else key_sb[g][:, t, :]
+                words = src.bitcast(F32)
+                for u in range(2):
+                    PE.transpose(v[:, i, u, :], words[:, u::2], ident[:])
+            trb[what, g, h] = b
+
+        grp = {}
+
+        def co(what, g, h, eng):
+            if h == 0:
+                grp[what, g] = work.tile([P, G, J], BF16, name="grp", tag="grp", bufs=3, align_bytes=64)
+            dst = grp[what, g][:].rearrange("p n j -> p (n j)").bitcast(F32)[:, h * 512 : h * 512 + 512]
+            dst = dst.rearrange("p (i r u) -> p i r u", i=2, u=2)
+            src = trb[what, g, h][:].rearrange("p (i u r) -> p i r u", i=2, u=2)
+            if eng is V:
+                V.tensor_copy(out=dst, in_=src)
+            else:
+                S.copy(dst, src)
+
+        def q1(what, g):
+            c, sc = (mq, ms) if what == "m" else (kq, ks)
+            V.quantize_mx(out=c[:, g, :].bitcast(FP8X4), scales=sc[:, g, :], in_=grp[what, g][:].rearrange("p n j -> p (n j)"))
+
+        clb = {}
+
+        def cl(i, c):
+            b = bank((i % 2) * 4 + c, "cl")
+            tg, t = divmod(i, J)
+            PE.matmul_mx(
+                out=b[:],
+                lhsT=kq[:, tg, t * P : t * P + P].bitcast(FP8X4),
+                lhsT_scale=ks[:, tg, t * P : t * P + P],
+                rhs=mq[:, c, :].bitcast(FP8X4),
+                rhs_scale=ms[:, c, :],
+                start=True,
+                stop=True,
+            )
+            clb[i, c] = b
+
+        def rmax(i, c):
+            V.tensor_reduce(out=mx[:, i, c : c + 1], in_=clb[i, c][:], axis=AX.X, op=ALU.max)
+
+        def nm(i):
+            V.tensor_reduce(out=nmax[:, i : i + 1], in_=mx[:, i, :], axis=AX.X, op=ALU.max, negate=True)
+
+        def ex(i, cs=range(NG)):
+            tg, t = divmod(i, J)
+            for c in cs:
+                S.activation(out=e_sb[tg][:, t, c * G : c * G + G], in_=clb[i, c][:], func=ACT.Exp, bias=nmax[:, i : i + 1], accum_out=sums[:, i, c : c + 1])
+
+        eag = {}
+
+        def prep(x, g, eng):
+            d = work.tile([P, W, J], BF16, name="eag", tag="eag", bufs=2, align_bytes=64)
+            src = ea_sb[x, g][:].rearrange("p t w -> p w t")
+            if eng is V:
+                V.tensor_copy(out=d[:], in_=src)
+            elif eng is S:
+                S.copy(d[:], src)
+            else:
+                for w0 in range(0, W, 128):
+                    GP.tensor_scalar(out=d[:, w0 : w0 + 128, :], in0=src[:, w0 : w0 + 128, :], scalar1=1.0, scalar2=0.0, op0=ALU.mult, op1=ALU.add)
+            eag[x, g] = d
+
+        def prepq(x, g):
+            V.quantize_mx(out=eq[x, g][:].bitcast(FP8X4), scales=es[x, g][:], in_=eag[x, g][:].rearrange("p w t -> p (w t)"))
+
+        def cf1(tg):
+            V.tensor_reduce(out=tot[:, tg, :], in_=sums[:, tg * J : tg * J + J, :], axis=AX.X, op=ALU.add)
+
+        def cf2(tg):
+            V.reciprocal(rtot[:, tg, :], tot[:, tg, :])
+
+        def cf3(tg):
+            V.scalar_tensor_tensor(out=coef[:, tg, :], in0=s_sb[:, tg, :], scalar=64.0, in1=rtot[:, tg, :], op0=ALU.mult, op1=ALU.mult)
+
+        def cf(tg):
+            V.tensor_reduce(out=tot[:, tg, :], in_=sums[:, tg * J : tg * J + J, :], axis=AX.X, op=ALU.add)
+            V.reciprocal(rtot[:, tg, :], tot[:, tg, :])
+            V.scalar_tensor_tensor(out=coef[:, tg, :], in0=s_sb[:, tg, :], scalar=64.0, in1=rtot[:, tg, :], op0=ALU.mult, op1=ALU.mult)
+
+        wsb = {}
+        w16 = {}
+
+        def wscale(tg, c):
+            d = work.tile([P, J, G], BF16, name="wsb", tag="wsb", bufs=2, align_bytes=64)
+            for t in range(J):
+                S.activation(out=d[:, t, :], in_=e_sb[tg][:, t, c * G : c * G + G], func=ACT.Copy, scale=coef[:, tg, t : t + 1])
+            wsb[tg, c] = d
+
+        def wil(tg, c, eng=V):
+            d = work.tile([P, G, J], BF16, name="w16", tag="w16", bufs=3, align_bytes=64)
+            if (tg, c) in wsb:
+                V.tensor_copy(out=d[:], in_=wsb[tg, c][:].rearrange("p t n -> p n t"))
+            else:
+                step = G if eng is V else 128
+                for n0 in range(0, G, step):
+                    eng.tensor_tensor(
+                        out=d[:, n0 : n0 + step, :],
+                        in0=e_sb[tg][:, :, c * G + n0 : c * G + n0 + step].rearrange("p t n -> p n t"),
+                        in1=coef[:, tg, :].unsqueeze(1).to_broadcast([P, step, J]),
+                        op=ALU.mult,
+                    )
+            w16[tg, c] = d
+
+        def wqz(tg, c):
+            cols = slice(c * G, c * G + G)
+            V.quantize_mx(out=wq[tg][:, cols].bitcast(FP8X4), scales=wsc[tg][:, cols], in_=w16[tg, c][:].rearrange("p n t -> p (n t)"))
+
+        eb = {}
+        o32 = {}
+
+        pos = []
+
+        def mm2(x, j):
+            g, t = divmod(j, J)
+            cols = slice(g * G + t * P, g * G + t * P + P)
+            b = bank(len(pos) % 8, "mm2")
+            pos.append(1)
+            for tg in range(TG):
+                PE.matmul_mx(
+                    out=b[:],
+                    lhsT=wq[tg][:, cols].bitcast(FP8X4),
+                    lhsT_scale=wsc[tg][:, cols],
+                    rhs=eq[x, tg][:].bitcast(FP8X4),
+                    rhs_scale=es[x, tg][:],
+                    start=(tg == 0),
+                    stop=(tg == TG - 1),
+                )
+            eb[x, j] = b
+
+        ab = {}
+
+        def ea(j):
+            g, t = divmod(j, J)
+            a = work.tile([P, W], F32, name="a", tag="a", bufs=4)
+            V.scalar_tensor_tensor(out=a[:], in0=eb["er", j][:], scalar=1.0, in1=mem_sb[g][:, t, :], op0=ALU.subtract, op1=ALU.mult)
+            ab[j] = (a, ALU.subtract)
+
+        def ef(j):
+            g, t = divmod(j, J)
+            f = work.tile([P, W], F32, name="f", tag="f", bufs=3)
+            S.activation(out=f[:], in_=eb["er", j][:], func=ACT.Copy, scale=-1.0, bias=1.0)
+            a = work.tile([P, W], F32, name="a", tag="a", bufs=4)
+            GP.tensor_tensor(out=a[:], in0=f[:], in1=mem_sb[g][:, t, :], op=ALU.mult)
+            ab[j] = (a, ALU.add)
+
+        def eo(j):
+            g, t = divmod(j, J)
+            if j == 0:
+                o_all = keep.tile([P, NG, J, W], F32, name="o32", tag="e0", align_bytes=64)
+                for gg in range(NG):
+                    o32[gg] = o_all[:, gg, :, :]
+            a, op = ab[j]
+            V.tensor_tensor(out=o32[g][:, t, :], in0=eb["ad", j][:], in1=a[:], op=op)
+            if t % 2 == 1:
+                nc.sync.dma_start(out=rows(out_0, g)[:, t - 1 : t + 1, :], in_=o32[g][:, t - 1 : t + 1, :])
+
+        o16 = {}
+
+        def oi(g, h, eng):
+            d = work.tile([P, 256, J], BF16, name="o16", tag="o16", bufs=3, align_bytes=64)
+            src = o32[g][:, :, h * 256 : h * 256 + 256].rearrange("p t w -> p w t")
+            if eng is V:
+                V.tensor_copy(out=d[:], in_=src)
+            else:
+                S.copy(d[:], src)
+            o16[g, h] = d
+
+        oc = {}
+
+        def oq(g, h):
+            if h == 0:
+                oc[g] = (work.tile([P, W], U32, name="oc", tag="oc", align_bytes=64), work.tile([P, W], U8, name="os", tag="os", align_bytes=64))
+            c, sc = oc[g]
+            cols = slice(h * 256, h * 256 + 256)
+            V.quantize_mx(out=c[:, cols].bitcast(FP8X4), scales=sc[:, cols], in_=o16[g, h][:].rearrange("p w t -> p (w t)"))
+            if h == 1:
+                nc.sync.dma_start(out=out_1[g].rearrange("p m t -> p (m t)").bitcast(I32), in_=c[:].bitcast(I32))
+                for q in range(4):
+                    nc.sync.dma_start(out=out_2[g, 4 * q : 4 * q + 4, :].bitcast(I32), in_=sc[32 * q : 32 * q + 4, :].bitcast(I32))
+
+        R4 = range(J)
+        C4 = range(NG)
+        gm_bcast()
+        tr("k", 0, 0, 0)
+        tr("k", 0, 1, 1)
+        sq(0, (0, 1))
+        sqv(0, (2, 3))
+        rn(0)
+        gm_copy()
+        co("k", 0, 0, V)
+        mn(0, R4)
+        co("k", 0, 1, S)
+        sq(1, R4)
+        rn(1)
+        q1("k", 0)
+        tr("m", 0, 0, 2)
+        tr("m", 0, 1, 3)
+        tr("k", 1, 0, 4)
+        tr("k", 1, 1, 5)
+        co("m", 0, 0, S)
+        co("m", 0, 1, V)
+        sq(2, R4)
+        rn(2)
+        mn(1, (0, 1))
+        q1("m", 0)
+        mn(1, (2, 3))
+        co("k", 1, 0, S)
+        tr("m", 1, 0, 6)
+        tr("m", 1, 1, 0)
+        sq(3, R4)
+        rn(3)
+        co("k", 1, 1, S)
+        co("m", 1, 0, S)
+        co("m", 1, 1, S)
+        mn(2, R4)
+        q1("k", 1)
+        mn(3, R4)
+        q1("m", 1)
+        tr("m", 2, 0, 2)
+        tr("m", 2, 1, 3)
+        co("m", 2, 0, S)
+        co("m", 2, 1, V)
+        tr("m", 3, 0, 6)
+        tr("m", 3, 1, 7)
+        prep("er", 0, S)
+        prep("ad", 0, S)
+        cl(0, 0)
+        cl(0, 1)
+        rmax(0, 0)
+        q1("m", 2)
+        rmax(0, 1)
+        co("m", 3, 0, S)
+        co("m", 3, 1, S)
+        cl(1, 0)
+        cl(1, 1)
+        cl(0, 2)
+        cl(1, 2)
+        rmax(1, 0)
+        rmax(1, 1)
+        rmax(0, 2)
+        q1("m", 3)
+        rmax(1, 2)
+        cl(0, 3)
+        cl(1, 3)
+        rmax(0, 3)
+        rmax(1, 3)
+        nm(0)
+        ex(0)
+        prepq("er", 0)
+        nm(1)
+        ex(1)
+        prepq("ad", 0)
+        prep("er", 1, S)
+        prep("ad", 1, S)
+        for i in range(2, 5):
+            for c in C4:
+                cl(i, c)
+            for c in C4:
+                rmax(i, c)
+                if i > 2 and c == 0:
+                    nm(i - 1)
+                    ex(i - 1)
+        cl(5, 0)
+        cl(5, 1)
+        cl(5, 2)
+        cl(5, 3)
+        prepq("er", 1)
+        nm(4)
+        ex(4)
+        cf1(0)
+        rmax(5, 0)
+        cf2(0)
+        rmax(5, 1)
+        cf3(0)
+        rmax(5, 2)
+        rmax(5, 3)
+        wscale(0, 0)
+        wil(0, 3)
+        for c in C4:
+            cl(6, c)
+        rmax(6, 0)
+        nm(5)
+        ex(5)
+        rmax(6, 1)
+        rmax(6, 2)
+        rmax(6, 3)
+        wscale(0, 1)
+        wil(0, 0)
+        nm(6)
+        ex(6)
+        for c in C4:
+            cl(7, c)
+        rmax(7, 0)
+        wqz(0, 0)
+        rmax(7, 1)
+        rmax(7, 2)
+        rmax(7, 3)
+        wil(0, 1)
+        nm(7)
+        ex(7)
+        prepq("ad", 1)
+        wqz(0, 1)
+        wqz(0, 3)
+        wil(0, 2)
+        cf1(1)
+        wqz(0, 2)
+        cf2(1)
+        cf3(1)
+        EF = (1, 3, 5, 7, 9, 11, 13, 15,)
+        extra = {
+            0: [lambda: wil(1, 1), lambda: wqz(1, 1)],
+            2: [lambda: wil(1, 2), lambda: wqz(1, 2)],
+            3: [lambda: wscale(1, 3)],
+            5: [lambda: wil(1, 3), lambda: wqz(1, 3)],
+        }
+        wil(1, 0)
+        wscale(1, 1)
+        wqz(1, 0)
+        mm2("er", 0)
+        wscale(1, 2)
+        for j in range(NG * J):
+            if j + 1 < NG * J:
+                if (j + 1) % J:
+                    mm2("er", j + 1)
+            mm2("ad", j)
+            if j in EF:
+                ef(j)
+            else:
+                ea(j)
+            if j > 0:
+                eo(j - 1)
+            for fn in extra.get(j, []):
+                fn()
+            if j + 1 < NG * J and (j + 1) % J == 0:
+                mm2("er", j + 1)
+            g, t = divmod(j, J)
+            if g > 0 and t == 1:
+                oi(g - 1, 0, S)
+            if g > 0 and t == 2:
+                oi(g - 1, 1, S)
+                oq(g - 1, 0)
+            if g > 0 and t == 3:
+                oq(g - 1, 1)
+        eo(NG * J - 1)
+        oi(NG - 1, 0, S)
+        oi(NG - 1, 1, V)
+        oq(NG - 1, 0)
+        oq(NG - 1, 1)

@@ -26,6 +26,7 @@ def tile_ntmcontentaddresseraseadd_x1_kernel(tc, key, mem, gm, s, erase, add, ou
         keep = ctx.enter_context(tc.tile_pool(name="keep", bufs=1))
         work = ctx.enter_context(tc.tile_pool(name="work", bufs=2))
         psum = ctx.enter_context(tc.psum_pool(name="psum", bufs=1))
+        ctx.enter_context(tc.manual_schedule())
 
         def rows(x, g):
             return x.rearrange("(g p t) w -> g p t w", p=P, t=J)[g]
@@ -73,17 +74,17 @@ def tile_ntmcontentaddresseraseadd_x1_kernel(tc, key, mem, gm, s, erase, add, ou
 
         V.memset(gm_row[:], 0.0)
         V.memset(ones[:], 1.0)
-        GP.dma_start(out=gm_row[0:1, :], in_=gm.rearrange("(o w) -> o w", o=1))
-        GP.dma_start(out=s_sb[:], in_=s.rearrange("(g p t) -> p g t", p=P, t=J))
         make_identity(nc, ident[:])
         GP.memset(mhalf[:], -0.5)
         nc.sync.dma_start(out=mem_sb[0][:, 0:2, :], in_=rows(mem, 0)[:, 0:2, :])
+        nc.sync.dma_start(out=gm_row[0:1, :], in_=gm.rearrange("(o w) -> o w", o=1))
         nc.sync.dma_start(out=mem_sb[0][:, 2:4, :], in_=rows(mem, 0)[:, 2:4, :])
         nc.sync.dma_start(out=key_sb[0][:], in_=rows(key, 0))
         nc.sync.dma_start(out=mem_sb[1][:], in_=rows(mem, 1))
-        nc.sync.dma_start(out=key_sb[1][:], in_=rows(key, 1))
         nc.sync.dma_start(out=mem_sb[2][:], in_=rows(mem, 2))
         nc.sync.dma_start(out=mem_sb[3][:], in_=rows(mem, 3))
+        nc.sync.dma_start(out=key_sb[1][:], in_=rows(key, 1))
+        nc.sync.dma_start(out=s_sb[:], in_=s.rearrange("(g p t) -> p g t", p=P, t=J))
         for g in range(TG):
             nc.sync.dma_start(out=ea_sb["er", g][:], in_=rows(erase, g))
             nc.sync.dma_start(out=ea_sb["ad", g][:], in_=rows(add, g))
@@ -148,7 +149,7 @@ def tile_ntmcontentaddresseraseadd_x1_kernel(tc, key, mem, gm, s, erase, add, ou
         grp = {}
 
         def co(what, g, h, eng):
-            if h == 0:
+            if (what, g) not in grp:
                 grp[what, g] = work.tile([P, G, J], BF16, name="grp", tag="grp", bufs=3, align_bytes=64)
             dst = grp[what, g][:].rearrange("p n j -> p (n j)").bitcast(F32)[:, h * 512 : h * 512 + 512]
             dst = dst.rearrange("p (i r u) -> p i r u", i=2, u=2)
@@ -190,6 +191,12 @@ def tile_ntmcontentaddresseraseadd_x1_kernel(tc, key, mem, gm, s, erase, add, ou
                 S.activation(out=e_sb[tg][:, t, c * G : c * G + G], in_=clb[i, c][:], func=ACT.Exp, bias=nmax[:, i : i + 1], accum_out=sums[:, i, c : c + 1])
 
         eag = {}
+
+        def prepg(x, g, k):
+            if (x, g) not in eag:
+                eag[x, g] = work.tile([P, W, J], BF16, name="eag", tag="eag", bufs=2, align_bytes=64)
+            c = slice(128 * k, 128 * k + 128)
+            GP.tensor_scalar(out=eag[x, g][:, c, :], in0=ea_sb[x, g][:, :, c].rearrange("p t w -> p w t"), scalar1=1.0, scalar2=0.0, op0=ALU.mult, op1=ALU.add)
 
         def prep(x, g, eng):
             d = work.tile([P, W, J], BF16, name="eag", tag="eag", bufs=2, align_bytes=64)
@@ -244,6 +251,26 @@ def tile_ntmcontentaddresseraseadd_x1_kernel(tc, key, mem, gm, s, erase, add, ou
                     )
             w16[tg, c] = d
 
+        def wilg(tg, c, k):
+            if (tg, c) not in w16:
+                w16[tg, c] = work.tile([P, G, J], BF16, name="w16", tag="w16", bufs=3, align_bytes=64)
+            n0 = 128 * k
+            GP.tensor_tensor(
+                out=w16[tg, c][:, n0 : n0 + 128, :],
+                in0=e_sb[tg][:, :, c * G + n0 : c * G + n0 + 128].rearrange("p t n -> p n t"),
+                in1=coef[:, tg, :].unsqueeze(1).to_broadcast([P, 128, J]),
+                op=ALU.mult,
+            )
+
+        def wscale1(tg, c, t):
+            if (tg, c) not in wsb:
+                wsb[tg, c] = work.tile([P, J, G], BF16, name="wsb", tag="wsb", bufs=2, align_bytes=64)
+            S.activation(out=wsb[tg, c][:, t, :], in_=e_sb[tg][:, t, c * G : c * G + G], func=ACT.Copy, scale=coef[:, tg, t : t + 1])
+
+        def ex1(i, c):
+            tg, t = divmod(i, J)
+            S.activation(out=e_sb[tg][:, t, c * G : c * G + G], in_=clb[i, c][:], func=ACT.Exp, bias=nmax[:, i : i + 1], accum_out=sums[:, i, c : c + 1])
+
         def wqz(tg, c):
             cols = slice(c * G, c * G + G)
             V.quantize_mx(out=wq[tg][:, cols].bitcast(FP8X4), scales=wsc[tg][:, cols], in_=w16[tg, c][:].rearrange("p n t -> p (n t)"))
@@ -271,6 +298,8 @@ def tile_ntmcontentaddresseraseadd_x1_kernel(tc, key, mem, gm, s, erase, add, ou
             eb[x, j] = b
 
         ab = {}
+        fb = {}
+        done = {}
 
         def ea(j):
             g, t = divmod(j, J)
@@ -282,22 +311,30 @@ def tile_ntmcontentaddresseraseadd_x1_kernel(tc, key, mem, gm, s, erase, add, ou
             g, t = divmod(j, J)
             f = work.tile([P, W], F32, name="f", tag="f", bufs=3)
             S.activation(out=f[:], in_=eb["er", j][:], func=ACT.Copy, scale=-1.0, bias=1.0)
+            fb[j] = f
+
+        def em(j):
+            g, t = divmod(j, J)
+            f = fb[j]
             a = work.tile([P, W], F32, name="a", tag="a", bufs=4)
             GP.tensor_tensor(out=a[:], in0=f[:], in1=mem_sb[g][:, t, :], op=ALU.mult)
             ab[j] = (a, ALU.add)
 
         def eo(j):
             g, t = divmod(j, J)
-            if j == 0:
+            if 0 not in o32:
                 o_all = keep.tile([P, NG, J, W], F32, name="o32", tag="e0", align_bytes=64)
                 for gg in range(NG):
                     o32[gg] = o_all[:, gg, :, :]
             a, op = ab[j]
             V.tensor_tensor(out=o32[g][:, t, :], in0=eb["ad", j][:], in1=a[:], op=op)
-            if t % 2 == 1:
+            done[j] = True
+            if (j ^ 1) in done:
+                t |= 1
                 nc.sync.dma_start(out=rows(out_0, g)[:, t - 1 : t + 1, :], in_=o32[g][:, t - 1 : t + 1, :])
 
         o16 = {}
+        done_q = {}
 
         def oi(g, h, eng):
             d = work.tile([P, 256, J], BF16, name="o16", tag="o16", bufs=3, align_bytes=64)
@@ -311,181 +348,341 @@ def tile_ntmcontentaddresseraseadd_x1_kernel(tc, key, mem, gm, s, erase, add, ou
         oc = {}
 
         def oq(g, h):
-            if h == 0:
+            if g not in oc:
                 oc[g] = (work.tile([P, W], U32, name="oc", tag="oc", align_bytes=64), work.tile([P, W], U8, name="os", tag="os", align_bytes=64))
             c, sc = oc[g]
             cols = slice(h * 256, h * 256 + 256)
             V.quantize_mx(out=c[:, cols].bitcast(FP8X4), scales=sc[:, cols], in_=o16[g, h][:].rearrange("p w t -> p (w t)"))
-            if h == 1:
+            done_q[g, h] = True
+            if (g, 1 - h) in done_q:
                 nc.sync.dma_start(out=out_1[g].rearrange("p m t -> p (m t)").bitcast(I32), in_=c[:].bitcast(I32))
                 for q in range(4):
                     nc.sync.dma_start(out=out_2[g, 4 * q : 4 * q + 4, :].bitcast(I32), in_=sc[32 * q : 32 * q + 4, :].bitcast(I32))
 
-        R4 = range(J)
-        C4 = range(NG)
+        sq(0, (0,))
+        sqv(0, (2,))
         gm_bcast()
-        tr("k", 0, 0, 0)
-        tr("k", 0, 1, 1)
-        sq(0, (0, 1))
-        sqv(0, (2, 3))
-        rn(0)
         gm_copy()
-        co("k", 0, 0, V)
-        mn(0, R4)
-        co("k", 0, 1, S)
-        sq(1, R4)
-        rn(1)
-        q1("k", 0)
+        sq(0, (1,))
+        tr("k", 0, 0, 0)
+        sqv(0, (3,))
+        rn(0)
+        mn(0, (0,))
+        mn(0, (1,))
+        mn(0, (2,))
+        sqv(1, (3,))
+        sqv(2, (3,))
+        co("k", 0, 0, S)
+        sq(1, (0,))
+        sq(1, (1,))
+        sq(1, (2,))
         tr("m", 0, 0, 2)
-        tr("m", 0, 1, 3)
-        tr("k", 1, 0, 4)
-        tr("k", 1, 1, 5)
-        co("m", 0, 0, S)
-        co("m", 0, 1, V)
-        sq(2, R4)
+        rn(1)
+        mn(0, (3,))
+        tr("k", 0, 1, 1)
+        sq(2, (0,))
+        sq(2, (1,))
+        mnx(3, (1,))
+        co("k", 0, 1, S)
+        sq(2, (2,))
         rn(2)
-        mn(1, (0, 1))
-        q1("m", 0)
-        mn(1, (2, 3))
-        co("k", 1, 0, S)
+        mn(1, (0,))
+        q1("k", 0)
+        sq(3, (0,))
+        sq(3, (1,))
+        sq(3, (2,))
+        sq(3, (3,))
+        mn(1, (1,))
+        mn(1, (2,))
+        co("m", 0, 0, S)
+        tr("m", 0, 1, 3)
+        mn(1, (3,))
+        tr("m", 1, 1, 5)
+        mn(2, (0,))
+        mn(2, (1,))
+        co("m", 0, 1, S)
+        prepg("er", 0, 0)
         tr("m", 1, 0, 6)
-        tr("m", 1, 1, 0)
-        sq(3, R4)
-        rn(3)
-        co("k", 1, 1, S)
-        co("m", 1, 0, S)
-        co("m", 1, 1, S)
-        mn(2, R4)
-        q1("k", 1)
-        mn(3, R4)
-        q1("m", 1)
         tr("m", 2, 0, 2)
+        co("m", 1, 0, S)
+        mn(2, (2,))
+        mn(2, (3,))
         tr("m", 2, 1, 3)
-        co("m", 2, 0, S)
-        co("m", 2, 1, V)
-        tr("m", 3, 0, 6)
-        tr("m", 3, 1, 7)
-        prep("er", 0, S)
-        prep("ad", 0, S)
+        q1("m", 0)
         cl(0, 0)
-        cl(0, 1)
+        prepg("er", 0, 2)
+        prepg("er", 0, 1)
+        rn(3)
+        mn(3, (0,))
+        mns(3, (1,))
+        tr("m", 3, 0, 6)
+        tr("k", 1, 0, 1)
+        co("m", 1, 1, S)
+        co("m", 2, 0, S)
+        co("m", 2, 1, S)
         rmax(0, 0)
+        q1("m", 1)
         q1("m", 2)
-        rmax(0, 1)
-        co("m", 3, 0, S)
-        co("m", 3, 1, S)
-        cl(1, 0)
-        cl(1, 1)
+        cl(0, 1)
+        mnx(3, (2,))
+        mns(3, (2,))
+        mnx(3, (3,))
         cl(0, 2)
-        cl(1, 2)
-        rmax(1, 0)
-        rmax(1, 1)
+        rmax(0, 1)
+        prepg("er", 0, 3)
         rmax(0, 2)
-        q1("m", 3)
-        rmax(1, 2)
-        cl(0, 3)
-        cl(1, 3)
-        rmax(0, 3)
-        rmax(1, 3)
-        nm(0)
-        ex(0)
+        mns(3, (3,))
+        prepg("ad", 0, 0)
+        tr("m", 3, 1, 4)
+        co("m", 3, 0, S)
+        co("k", 1, 0, S)
         prepq("er", 0)
+        co("m", 3, 1, S)
+        q1("m", 3)
+        tr("k", 1, 1, 5)
+        prepg("er", 1, 0)
+        prepg("ad", 0, 3)
+        cl(1, 0)
+        co("k", 1, 1, S)
+        cl(1, 1)
+        prepg("ad", 0, 2)
+        rmax(1, 1)
+        cl(0, 3)
+        rmax(0, 3)
+        rmax(1, 0)
+        nm(0)
+        ex1(0, 0)
+        ex1(0, 3)
+        cl(1, 3)
+        cl(1, 2)
+        rmax(1, 2)
+        cl(2, 0)
+        ex1(0, 1)
+        rmax(1, 3)
+        rmax(2, 0)
         nm(1)
-        ex(1)
+        prepg("ad", 0, 1)
+        cl(2, 3)
+        rmax(2, 3)
+        cl(2, 1)
+        rmax(2, 1)
+        ex1(0, 2)
+        cl(2, 2)
+        ex1(1, 3)
+        cl(3, 3)
+        rmax(2, 2)
+        rmax(3, 3)
+        nm(2)
+        ex1(1, 1)
+        cl(3, 1)
+        ex1(1, 0)
+        rmax(3, 1)
+        cl(3, 0)
+        rmax(3, 0)
+        ex1(1, 2)
+        cl(3, 2)
+        ex1(2, 3)
+        ex1(2, 2)
+        rmax(3, 2)
+        q1("k", 1)
+        prepg("er", 1, 1)
+        ex1(2, 1)
+        nm(3)
+        ex1(2, 0)
+        cl(4, 3)
         prepq("ad", 0)
-        prep("er", 1, S)
-        prep("ad", 1, S)
-        for i in range(2, 5):
-            for c in C4:
-                cl(i, c)
-            for c in C4:
-                rmax(i, c)
-                if i > 2 and c == 0:
-                    nm(i - 1)
-                    ex(i - 1)
-        cl(5, 0)
-        cl(5, 1)
+        rmax(4, 3)
+        prepg("er", 1, 2)
+        cl(4, 2)
+        rmax(4, 2)
+        ex1(3, 1)
+        cl(4, 1)
+        rmax(4, 1)
+        ex1(3, 2)
+        prepg("ad", 1, 0)
+        ex1(3, 3)
+        cl(4, 0)
+        rmax(4, 0)
         cl(5, 2)
-        cl(5, 3)
-        prepq("er", 1)
-        nm(4)
-        ex(4)
+        ex1(3, 0)
         cf1(0)
-        rmax(5, 0)
-        cf2(0)
+        nm(4)
+        ex1(4, 0)
+        ex1(4, 2)
+        prepg("ad", 1, 1)
+        cl(5, 1)
         rmax(5, 1)
-        cf3(0)
-        rmax(5, 2)
+        cf2(0)
+        cl(5, 3)
         rmax(5, 3)
-        wscale(0, 0)
-        wil(0, 3)
-        for c in C4:
-            cl(6, c)
-        rmax(6, 0)
+        cf3(0)
+        wscale1(0, 0, 0)
+        wscale1(0, 0, 3)
+        prepg("er", 1, 3)
+        wscale1(0, 0, 2)
+        wscale1(0, 0, 1)
+        ex1(4, 3)
+        cl(5, 0)
+        rmax(5, 0)
+        cl(6, 3)
+        rmax(5, 2)
+        cl(6, 2)
+        prepg("ad", 1, 2)
+        prepq("er", 1)
         nm(5)
-        ex(5)
-        rmax(6, 1)
-        rmax(6, 2)
-        rmax(6, 3)
-        wscale(0, 1)
-        wil(0, 0)
-        nm(6)
-        ex(6)
-        for c in C4:
-            cl(7, c)
-        rmax(7, 0)
-        wqz(0, 0)
-        rmax(7, 1)
-        rmax(7, 2)
-        rmax(7, 3)
-        wil(0, 1)
-        nm(7)
-        ex(7)
+        ex1(5, 3)
+        ex1(5, 0)
+        prepg("ad", 1, 3)
         prepq("ad", 1)
-        wqz(0, 1)
-        wqz(0, 3)
+        wil(0, 0)
+        wqz(0, 0)
+        ex1(5, 1)
+        ex1(4, 1)
+        cl(6, 1)
+        cl(6, 0)
+        ex1(5, 2)
+        cl(7, 2)
+        cl(7, 1)
+        rmax(6, 3)
+        wscale1(0, 1, 0)
+        wscale1(0, 1, 2)
+        wscale1(0, 1, 1)
+        rmax(6, 2)
+        cl(7, 0)
+        rmax(6, 1)
+        wscale1(0, 1, 3)
+        rmax(6, 0)
+        rmax(7, 2)
+        nm(6)
+        ex1(6, 3)
+        ex1(6, 2)
+        rmax(7, 0)
+        ex1(6, 0)
+        cl(7, 3)
+        rmax(7, 3)
+        rmax(7, 1)
+        nm(7)
+        ex1(6, 1)
+        ex1(7, 2)
+        wil(0, 1)
         wil(0, 2)
+        ex1(7, 1)
+        wilg(0, 3, 0)
+        wilg(0, 3, 3)
+        wilg(0, 3, 2)
+        ex1(7, 0)
+        ex1(7, 3)
         cf1(1)
-        wqz(0, 2)
+        wqz(0, 1)
         cf2(1)
+        wqz(0, 2)
         cf3(1)
-        EF = (1, 3, 5, 7, 9, 11, 13, 15,)
-        extra = {
-            0: [lambda: wil(1, 1), lambda: wqz(1, 1)],
-            2: [lambda: wil(1, 2), lambda: wqz(1, 2)],
-            3: [lambda: wscale(1, 3)],
-            5: [lambda: wil(1, 3), lambda: wqz(1, 3)],
-        }
+        wscale1(1, 1, 0)
+        wscale1(1, 1, 2)
+        wilg(0, 3, 1)
+        wscale1(1, 1, 3)
+        wqz(0, 3)
         wil(1, 0)
-        wscale(1, 1)
+        wscale1(1, 1, 1)
+        wil(1, 1)
         wqz(1, 0)
+        wscale1(1, 2, 0)
+        mm2("ad", 1)
+        mm2("ad", 0)
+        wscale1(1, 2, 1)
+        wqz(1, 1)
         mm2("er", 0)
-        wscale(1, 2)
-        for j in range(NG * J):
-            if j + 1 < NG * J:
-                if (j + 1) % J:
-                    mm2("er", j + 1)
-            mm2("ad", j)
-            if j in EF:
-                ef(j)
-            else:
-                ea(j)
-            if j > 0:
-                eo(j - 1)
-            for fn in extra.get(j, []):
-                fn()
-            if j + 1 < NG * J and (j + 1) % J == 0:
-                mm2("er", j + 1)
-            g, t = divmod(j, J)
-            if g > 0 and t == 1:
-                oi(g - 1, 0, S)
-            if g > 0 and t == 2:
-                oi(g - 1, 1, S)
-                oq(g - 1, 0)
-            if g > 0 and t == 3:
-                oq(g - 1, 1)
-        eo(NG * J - 1)
-        oi(NG - 1, 0, S)
-        oi(NG - 1, 1, V)
-        oq(NG - 1, 0)
-        oq(NG - 1, 1)
+        wscale1(1, 2, 3)
+        mm2("er", 1)
+        wscale1(1, 2, 2)
+        wil(1, 2)
+        mm2("er", 2)
+        ea(0)
+        wilg(1, 3, 0)
+        eo(0)
+        ef(1)
+        em(1)
+        mm2("er", 3)
+        ea(2)
+        mm2("ad", 2)
+        mm2("er", 4)
+        ef(3)
+        em(3)
+        ea(4)
+        mm2("ad", 4)
+        mm2("er", 5)
+        ef(5)
+        eo(1)
+        em(5)
+        mm2("er", 6)
+        mm2("er", 7)
+        wqz(1, 2)
+        mm2("er", 9)
+        ef(7)
+        eo(2)
+        ea(6)
+        ef(9)
+        mm2("ad", 3)
+        eo(3)
+        wilg(1, 3, 3)
+        mm2("ad", 6)
+        eo(6)
+        mm2("ad", 5)
+        em(7)
+        eo(4)
+        eo(5)
+        mm2("er", 11)
+        ef(11)
+        mm2("er", 8)
+        ea(8)
+        oi(0, 0, S)
+        mm2("ad", 7)
+        eo(7)
+        oi(0, 1, S)
+        oi(1, 0, S)
+        mm2("ad", 9)
+        wilg(1, 3, 1)
+        wilg(1, 3, 2)
+        mm2("er", 10)
+        em(9)
+        ea(10)
+        em(11)
+        oq(0, 0)
+        mm2("ad", 8)
+        wqz(1, 3)
+        mm2("ad", 10)
+        oq(0, 1)
+        mm2("er", 12)
+        oi(1, 1, S)
+        eo(8)
+        ea(12)
+        mm2("er", 13)
+        eo(9)
+        mm2("er", 15)
+        ef(13)
+        mm2("ad", 11)
+        ef(15)
+        eo(10)
+        eo(11)
+        mm2("er", 14)
+        mm2("ad", 12)
+        oq(1, 0)
+        em(13)
+        oq(1, 1)
+        mm2("ad", 13)
+        eo(12)
+        eo(13)
+        ea(14)
+        oi(2, 0, S)
+        oq(2, 0)
+        oi(2, 1, S)
+        oq(2, 1)
+        em(15)
+        mm2("ad", 14)
+        eo(14)
+        mm2("ad", 15)
+        eo(15)
+        oi(3, 0, S)
+        oi(3, 1, V)
+        oq(3, 0)
+        oq(3, 1)

@@ -309,7 +309,7 @@ def tile_ntmcontentaddresseraseadd_x1_kernel(tc, key, mem, gm, s, erase, add, ou
 
         def ef(j):
             g, t = divmod(j, J)
-            f = work.tile([P, W], F32, name="f", tag="f", bufs=3)
+            f = work.tile([P, W], F32, name="f", tag="f", bufs=2)
             S.activation(out=f[:], in_=eb["er", j][:], func=ACT.Copy, scale=-1.0, bias=1.0)
             fb[j] = f
 
@@ -334,355 +334,346 @@ def tile_ntmcontentaddresseraseadd_x1_kernel(tc, key, mem, gm, s, erase, add, ou
                 nc.sync.dma_start(out=rows(out_0, g)[:, t - 1 : t + 1, :], in_=o32[g][:, t - 1 : t + 1, :])
 
         o16 = {}
-        done_q = {}
+        oc = {}
+        left = {}
 
-        def oi(g, h, eng):
-            d = work.tile([P, 256, J], BF16, name="o16", tag="o16", bufs=3, align_bytes=64)
-            src = o32[g][:, :, h * 256 : h * 256 + 256].rearrange("p t w -> p w t")
+        def oi(g, c0, c1, eng):
+            d = work.tile([P, c1 - c0, J], BF16, name="o16", tag="o16", bufs=2, align_bytes=64)
+            src = o32[g][:, :, c0:c1].rearrange("p t w -> p w t")
             if eng is V:
                 V.tensor_copy(out=d[:], in_=src)
             else:
                 S.copy(d[:], src)
-            o16[g, h] = d
+            o16[g, c0] = d
 
-        oc = {}
-
-        def oq(g, h):
+        def oq(g, c0, c1):
             if g not in oc:
                 oc[g] = (work.tile([P, W], U32, name="oc", tag="oc", align_bytes=64), work.tile([P, W], U8, name="os", tag="os", align_bytes=64))
+                left[g] = W
             c, sc = oc[g]
-            cols = slice(h * 256, h * 256 + 256)
-            V.quantize_mx(out=c[:, cols].bitcast(FP8X4), scales=sc[:, cols], in_=o16[g, h][:].rearrange("p w t -> p (w t)"))
-            done_q[g, h] = True
-            if (g, 1 - h) in done_q:
+            V.quantize_mx(out=c[:, c0:c1].bitcast(FP8X4), scales=sc[:, c0:c1], in_=o16[g, c0][:].rearrange("p w t -> p (w t)"))
+            left[g] -= c1 - c0
+            if left[g] == 0:
                 nc.sync.dma_start(out=out_1[g].rearrange("p m t -> p (m t)").bitcast(I32), in_=c[:].bitcast(I32))
                 for q in range(4):
                     nc.sync.dma_start(out=out_2[g, 4 * q : 4 * q + 4, :].bitcast(I32), in_=sc[32 * q : 32 * q + 4, :].bitcast(I32))
 
         sq(0, (0,))
+        sq(0, (1,))
         sqv(0, (2,))
         gm_bcast()
         gm_copy()
-        sq(0, (1,))
         tr("k", 0, 0, 0)
+        co("k", 0, 0, S)
         sqv(0, (3,))
+        sqv(1, (3,))
+        sqv(2, (3,))
+        sq(1, (0,))
+        sq(1, (1,))
+        sq(1, (2,))
         rn(0)
         mn(0, (0,))
         mn(0, (1,))
         mn(0, (2,))
-        sqv(1, (3,))
-        sqv(2, (3,))
-        co("k", 0, 0, S)
-        sq(1, (0,))
-        sq(1, (1,))
-        sq(1, (2,))
-        tr("m", 0, 0, 2)
-        rn(1)
-        mn(0, (3,))
-        tr("k", 0, 1, 1)
         sq(2, (0,))
-        sq(2, (1,))
         mnx(3, (1,))
-        co("k", 0, 1, S)
+        sq(2, (1,))
         sq(2, (2,))
-        rn(2)
+        mn(0, (3,))
+        rn(1)
         mn(1, (0,))
-        q1("k", 0)
+        tr("m", 0, 0, 2)
+        mnx(3, (2,))
+        mn(1, (1,))
+        tr("k", 0, 1, 1)
+        co("k", 0, 1, S)
         sq(3, (0,))
         sq(3, (1,))
-        sq(3, (2,))
-        sq(3, (3,))
-        mn(1, (1,))
-        mn(1, (2,))
-        co("m", 0, 0, S)
-        tr("m", 0, 1, 3)
-        mn(1, (3,))
-        tr("m", 1, 1, 5)
-        mn(2, (0,))
-        mn(2, (1,))
-        co("m", 0, 1, S)
-        prepg("er", 0, 0)
+        rn(2)
+        mnx(3, (3,))
         tr("m", 1, 0, 6)
-        tr("m", 2, 0, 2)
-        co("m", 1, 0, S)
-        mn(2, (2,))
-        mn(2, (3,))
-        tr("m", 2, 1, 3)
-        q1("m", 0)
-        cl(0, 0)
-        prepg("er", 0, 2)
-        prepg("er", 0, 1)
+        tr("m", 0, 1, 3)
+        co("m", 0, 0, S)
+        co("m", 0, 1, S)
+        sq(3, (2,))
+        q1("k", 0)
+        sq(3, (3,))
         rn(3)
+        mn(1, (2,))
+        mn(1, (3,))
+        mn(2, (0,))
+        prepg("er", 0, 0)
+        prepg("ad", 0, 0)
+        prepg("ad", 0, 1)
+        q1("m", 0)
+        tr("k", 1, 0, 1)
+        tr("m", 1, 1, 5)
+        mn(2, (1,))
+        mn(2, (2,))
+        tr("m", 2, 0, 2)
+        mn(2, (3,))
+        co("m", 1, 0, S)
+        prepg("er", 0, 3)
+        co("m", 1, 1, S)
         mn(3, (0,))
         mns(3, (1,))
-        tr("m", 3, 0, 6)
-        tr("k", 1, 0, 1)
-        co("m", 1, 1, S)
         co("m", 2, 0, S)
-        co("m", 2, 1, S)
+        cl(0, 0)
         rmax(0, 0)
-        q1("m", 1)
+        tr("m", 2, 1, 3)
+        co("m", 2, 1, S)
         q1("m", 2)
-        cl(0, 1)
-        mnx(3, (2,))
+        tr("m", 3, 0, 6)
         mns(3, (2,))
-        mnx(3, (3,))
-        cl(0, 2)
-        rmax(0, 1)
-        prepg("er", 0, 3)
-        rmax(0, 2)
         mns(3, (3,))
-        prepg("ad", 0, 0)
+        q1("m", 1)
+        tr("k", 1, 1, 5)
         tr("m", 3, 1, 4)
         co("m", 3, 0, S)
-        co("k", 1, 0, S)
-        prepq("er", 0)
         co("m", 3, 1, S)
+        cl(0, 2)
+        rmax(0, 2)
         q1("m", 3)
-        tr("k", 1, 1, 5)
-        prepg("er", 1, 0)
-        prepg("ad", 0, 3)
-        cl(1, 0)
+        cl(0, 1)
+        rmax(0, 1)
+        cl(0, 3)
+        prepg("er", 0, 1)
+        rmax(0, 3)
+        co("k", 1, 0, S)
+        prepg("ad", 0, 2)
         co("k", 1, 1, S)
         cl(1, 1)
-        prepg("ad", 0, 2)
         rmax(1, 1)
-        cl(0, 3)
-        rmax(0, 3)
-        rmax(1, 0)
+        prepg("er", 0, 2)
+        cl(1, 2)
         nm(0)
+        rmax(1, 2)
         ex1(0, 0)
         ex1(0, 3)
         cl(1, 3)
-        cl(1, 2)
-        rmax(1, 2)
-        cl(2, 0)
-        ex1(0, 1)
         rmax(1, 3)
-        rmax(2, 0)
-        nm(1)
-        prepg("ad", 0, 1)
+        ex1(0, 2)
+        cl(1, 0)
+        rmax(1, 0)
+        ex1(0, 1)
         cl(2, 3)
+        prepq("er", 0)
+        prepg("ad", 0, 3)
+        prepg("er", 1, 0)
+        prepg("er", 1, 2)
+        nm(1)
+        ex1(1, 3)
         rmax(2, 3)
+        ex1(1, 2)
+        cl(2, 0)
+        cl(2, 2)
+        rmax(2, 2)
+        rmax(2, 0)
+        ex1(1, 1)
+        prepg("er", 1, 1)
         cl(2, 1)
         rmax(2, 1)
-        ex1(0, 2)
-        cl(2, 2)
-        ex1(1, 3)
-        cl(3, 3)
-        rmax(2, 2)
-        rmax(3, 3)
-        nm(2)
-        ex1(1, 1)
         cl(3, 1)
         ex1(1, 0)
-        rmax(3, 1)
-        cl(3, 0)
-        rmax(3, 0)
-        ex1(1, 2)
-        cl(3, 2)
-        ex1(2, 3)
-        ex1(2, 2)
-        rmax(3, 2)
-        q1("k", 1)
-        prepg("er", 1, 1)
-        ex1(2, 1)
-        nm(3)
-        ex1(2, 0)
-        cl(4, 3)
         prepq("ad", 0)
-        rmax(4, 3)
-        prepg("er", 1, 2)
-        cl(4, 2)
-        rmax(4, 2)
-        ex1(3, 1)
-        cl(4, 1)
-        rmax(4, 1)
-        ex1(3, 2)
+        cl(3, 3)
         prepg("ad", 1, 0)
-        ex1(3, 3)
+        prepg("ad", 1, 3)
+        cl(3, 0)
+        prepg("ad", 1, 2)
+        nm(2)
+        rmax(3, 1)
+        ex1(2, 1)
+        ex1(2, 2)
+        ex1(2, 0)
+        ex1(2, 3)
+        prepg("ad", 1, 1)
+        cl(3, 2)
+        rmax(3, 2)
+        rmax(3, 3)
+        rmax(3, 0)
+        nm(3)
+        ex1(3, 1)
+        ex1(3, 2)
+        q1("k", 1)
+        prepq("ad", 1)
         cl(4, 0)
         rmax(4, 0)
-        cl(5, 2)
         ex1(3, 0)
+        cl(5, 1)
+        cl(4, 3)
+        rmax(4, 3)
+        cl(4, 1)
+        cl(4, 2)
+        rmax(4, 1)
+        rmax(4, 2)
+        ex1(3, 3)
         cf1(0)
         nm(4)
+        cl(5, 2)
         ex1(4, 0)
-        ex1(4, 2)
-        prepg("ad", 1, 1)
-        cl(5, 1)
+        ex1(4, 3)
         rmax(5, 1)
         cf2(0)
-        cl(5, 3)
-        rmax(5, 3)
-        cf3(0)
-        wscale1(0, 0, 0)
-        wscale1(0, 0, 3)
-        prepg("er", 1, 3)
-        wscale1(0, 0, 2)
-        wscale1(0, 0, 1)
-        ex1(4, 3)
         cl(5, 0)
         rmax(5, 0)
-        cl(6, 3)
+        ex1(4, 2)
+        cf3(0)
+        wscale1(0, 0, 0)
+        wscale1(0, 0, 1)
+        cl(5, 3)
+        rmax(5, 3)
         rmax(5, 2)
-        cl(6, 2)
-        prepg("ad", 1, 2)
-        prepq("er", 1)
-        nm(5)
-        ex1(5, 3)
-        ex1(5, 0)
-        prepg("ad", 1, 3)
-        prepq("ad", 1)
-        wil(0, 0)
-        wqz(0, 0)
-        ex1(5, 1)
-        ex1(4, 1)
-        cl(6, 1)
         cl(6, 0)
+        ex1(4, 1)
+        cl(6, 2)
+        rmax(6, 0)
+        nm(5)
+        prepg("er", 1, 3)
+        prepq("er", 1)
+        rmax(6, 2)
+        cl(6, 1)
         ex1(5, 2)
-        cl(7, 2)
-        cl(7, 1)
+        rmax(6, 1)
+        ex1(5, 0)
+        cl(6, 3)
         rmax(6, 3)
+        wscale1(0, 0, 3)
+        wscale1(0, 0, 2)
+        ex1(5, 3)
+        ex1(5, 1)
         wscale1(0, 1, 0)
         wscale1(0, 1, 2)
-        wscale1(0, 1, 1)
-        rmax(6, 2)
-        cl(7, 0)
-        rmax(6, 1)
-        wscale1(0, 1, 3)
-        rmax(6, 0)
+        cl(7, 2)
         rmax(7, 2)
-        nm(6)
-        ex1(6, 3)
-        ex1(6, 2)
+        cl(7, 0)
         rmax(7, 0)
-        ex1(6, 0)
+        wil(0, 0)
         cl(7, 3)
         rmax(7, 3)
+        wscale1(0, 1, 1)
+        wscale1(0, 1, 3)
+        cl(7, 1)
         rmax(7, 1)
+        nm(6)
+        ex1(6, 0)
+        wqz(0, 0)
         nm(7)
-        ex1(6, 1)
-        ex1(7, 2)
+        ex1(7, 3)
+        ex1(7, 0)
+        ex1(6, 2)
         wil(0, 1)
         wil(0, 2)
+        ex1(6, 3)
+        wil(0, 3)
+        ex1(6, 1)
+        ex1(7, 2)
         ex1(7, 1)
-        wilg(0, 3, 0)
-        wilg(0, 3, 3)
-        wilg(0, 3, 2)
-        ex1(7, 0)
-        ex1(7, 3)
         cf1(1)
         wqz(0, 1)
         cf2(1)
-        wqz(0, 2)
         cf3(1)
         wscale1(1, 1, 0)
-        wscale1(1, 1, 2)
-        wilg(0, 3, 1)
-        wscale1(1, 1, 3)
-        wqz(0, 3)
-        wil(1, 0)
         wscale1(1, 1, 1)
+        wscale1(1, 1, 2)
+        wscale1(1, 1, 3)
+        wscale1(1, 2, 0)
+        wscale1(1, 2, 2)
+        wqz(0, 2)
+        wscale1(1, 2, 3)
+        wil(1, 0)
         wil(1, 1)
         wqz(1, 0)
-        wscale1(1, 2, 0)
-        mm2("ad", 1)
-        mm2("ad", 0)
-        wscale1(1, 2, 1)
-        wqz(1, 1)
         mm2("er", 0)
-        wscale1(1, 2, 3)
-        mm2("er", 1)
-        wscale1(1, 2, 2)
-        wil(1, 2)
+        mm2("ad", 1)
+        wscale1(1, 2, 1)
         mm2("er", 2)
-        ea(0)
-        wilg(1, 3, 0)
-        eo(0)
-        ef(1)
-        em(1)
-        mm2("er", 3)
-        ea(2)
-        mm2("ad", 2)
+        wscale1(1, 3, 0)
+        wqz(1, 1)
         mm2("er", 4)
+        wscale1(1, 3, 2)
+        wqz(0, 3)
+        wil(1, 2)
+        wqz(1, 2)
+        ea(0)
+        mm2("er", 1)
+        ef(1)
+        mm2("ad", 0)
+        mm2("er", 3)
+        mm2("er", 5)
+        mm2("ad", 2)
+        mm2("ad", 3)
+        em(1)
+        ea(2)
+        mm2("er", 6)
+        wscale1(1, 3, 3)
+        eo(0)
+        mm2("ad", 4)
         ef(3)
         em(3)
-        ea(4)
-        mm2("ad", 4)
-        mm2("er", 5)
-        ef(5)
         eo(1)
-        em(5)
-        mm2("er", 6)
-        mm2("er", 7)
-        wqz(1, 2)
-        mm2("er", 9)
-        ef(7)
+        wscale1(1, 3, 1)
+        ef(5)
         eo(2)
-        ea(6)
-        ef(9)
-        mm2("ad", 3)
-        eo(3)
-        wilg(1, 3, 3)
         mm2("ad", 6)
-        eo(6)
-        mm2("ad", 5)
-        em(7)
-        eo(4)
-        eo(5)
-        mm2("er", 11)
-        ef(11)
-        mm2("er", 8)
-        ea(8)
-        oi(0, 0, S)
+        eo(3)
         mm2("ad", 7)
-        eo(7)
-        oi(0, 1, S)
-        oi(1, 0, S)
-        mm2("ad", 9)
-        wilg(1, 3, 1)
-        wilg(1, 3, 2)
+        mm2("ad", 5)
+        mm2("er", 9)
+        oi(0, 0, 512, S)
+        ea(4)
+        em(5)
+        ea(6)
+        mm2("er", 8)
+        wil(1, 3)
+        eo(4)
+        mm2("er", 7)
+        ef(7)
+        ef(9)
         mm2("er", 10)
+        wqz(1, 3)
+        em(7)
+        mm2("er", 11)
+        oq(0, 0, 512)
+        mm2("er", 13)
+        ef(11)
+        mm2("ad", 8)
+        eo(5)
+        mm2("ad", 9)
+        ef(13)
+        ea(8)
+        mm2("er", 12)
+        eo(6)
+        mm2("ad", 10)
+        eo(7)
+        mm2("ad", 11)
         em(9)
         ea(10)
-        em(11)
-        oq(0, 0)
-        mm2("ad", 8)
-        wqz(1, 3)
-        mm2("ad", 10)
-        oq(0, 1)
-        mm2("er", 12)
-        oi(1, 1, S)
+        oi(1, 0, 512, S)
         eo(8)
-        ea(12)
-        mm2("er", 13)
-        eo(9)
-        mm2("er", 15)
-        ef(13)
-        mm2("ad", 11)
-        ef(15)
-        eo(10)
-        eo(11)
-        mm2("er", 14)
         mm2("ad", 12)
-        oq(1, 0)
+        eo(10)
+        em(11)
+        eo(11)
+        eo(9)
+        oi(2, 0, 512, S)
+        mm2("er", 14)
+        mm2("ad", 14)
+        ea(12)
         em(13)
-        oq(1, 1)
+        ea(14)
+        eo(14)
         mm2("ad", 13)
+        mm2("er", 15)
+        ef(15)
+        oq(1, 0, 512)
+        oq(2, 0, 512)
         eo(12)
         eo(13)
-        ea(14)
-        oi(2, 0, S)
-        oq(2, 0)
-        oi(2, 1, S)
-        oq(2, 1)
-        em(15)
-        mm2("ad", 14)
-        eo(14)
         mm2("ad", 15)
+        em(15)
         eo(15)
-        oi(3, 0, S)
-        oi(3, 1, V)
-        oq(3, 0)
-        oq(3, 1)
+        oi(3, 0, 256, S)
+        oi(3, 256, 512, V)
+        oq(3, 0, 256)
+        oq(3, 256, 512)

@@ -26,7 +26,6 @@ def tile_ntmcontentaddresseraseadd_x1_kernel(tc, key, mem, gm, s, erase, add, ou
         keep = ctx.enter_context(tc.tile_pool(name="keep", bufs=1))
         work = ctx.enter_context(tc.tile_pool(name="work", bufs=2))
         psum = ctx.enter_context(tc.psum_pool(name="psum", bufs=1))
-        ctx.enter_context(tc.manual_schedule())
 
         def rows(x, g):
             return x.rearrange("(g p t) w -> g p t w", p=P, t=J)[g]
@@ -45,12 +44,11 @@ def tile_ntmcontentaddresseraseadd_x1_kernel(tc, key, mem, gm, s, erase, add, ou
                 ea_sb[x, g] = keep_tile("%s%d" % (x, g), [P, J, W], BF16)
         gm_row = keep_tile("gm_row", [P, W], BF16)
         ones = keep_tile("ones", [P, P], BF16)
+        ones_in = keep_tile("ones_in", [P, P], BF16)
         s_sb = keep_tile("s_sb", [P, TG, J], BF16)
         ident = keep_tile("ident", [P, P], F32)
-        mhalf = keep_tile("mhalf", [P, J], F32)
         gm_b = keep_tile("gm_b", [P, W], F32)
         ssq = keep_tile("ssq", [P, NG, J], F32)
-        ssqe = keep_tile("ssqe", [P, NG, J], F32)
         rinv = keep_tile("rinv", [P, NG, J], F32)
         mq = keep_tile("mq", [P, NG, G], U32)
         ms = keep_tile("ms", [P, NG, G], U8)
@@ -73,9 +71,9 @@ def tile_ntmcontentaddresseraseadd_x1_kernel(tc, key, mem, gm, s, erase, add, ou
         coef = keep_tile("coef", [P, TG, J], F32)
 
         V.memset(gm_row[:], 0.0)
-        V.memset(ones[:], 1.0)
+        V.memset(ones_in[:], 1.0)
+        S.activation(out=ones[:], in_=ones_in[:], func=ACT.Abs_reciprocal_sqrt)
         make_identity(nc, ident[:])
-        GP.memset(mhalf[:], -0.5)
         nc.sync.dma_start(out=mem_sb[0][:, 0:2, :], in_=rows(mem, 0)[:, 0:2, :])
         nc.sync.dma_start(out=gm_row[0:1, :], in_=gm.rearrange("(o w) -> o w", o=1))
         nc.sync.dma_start(out=mem_sb[0][:, 2:4, :], in_=rows(mem, 0)[:, 2:4, :])
@@ -110,8 +108,7 @@ def tile_ntmcontentaddresseraseadd_x1_kernel(tc, key, mem, gm, s, erase, add, ou
                 V.scalar_tensor_tensor(out=junk[:], in0=mem_sb[g][:, t, :], scalar=1.0, in1=mem_sb[g][:, t, :], op0=ALU.mult, op1=ALU.mult, accum_out=ssq[:, g, t : t + 1])
 
         def rn(g):
-            GP.tensor_scalar(out=ssqe[:, g, :], in0=ssq[:, g, :], scalar1=1e-6, scalar2=1.0, op0=ALU.add, op1=ALU.mult)
-            GP.tensor_tensor(out=rinv[:, g, :], in0=ssqe[:, g, :], in1=mhalf[:], op=ALU.pow)
+            S.activation(out=rinv[:, g, :], in_=ssq[:, g, :], func=ACT.Abs_reciprocal_sqrt, bias=1e-6)
 
         mnr = {}
 
@@ -358,322 +355,324 @@ def tile_ntmcontentaddresseraseadd_x1_kernel(tc, key, mem, gm, s, erase, add, ou
                 for q in range(4):
                     nc.sync.dma_start(out=out_2[g, 4 * q : 4 * q + 4, :].bitcast(I32), in_=sc[32 * q : 32 * q + 4, :].bitcast(I32))
 
+        gm_bcast()
         sq(0, (0,))
         sq(0, (1,))
         sqv(0, (2,))
-        gm_bcast()
+        sqv(0, (3,))
+        rn(0)
         gm_copy()
         tr("k", 0, 0, 0)
+        tr("k", 0, 1, 1)
         co("k", 0, 0, S)
-        sqv(0, (3,))
-        sqv(1, (3,))
-        sqv(2, (3,))
-        sq(1, (0,))
-        sq(1, (1,))
-        sq(1, (2,))
-        rn(0)
+        co("k", 0, 1, S)
+        q1("k", 0)
         mn(0, (0,))
         mn(0, (1,))
         mn(0, (2,))
-        sq(2, (0,))
-        mnx(3, (1,))
-        sq(2, (1,))
-        sq(2, (2,))
         mn(0, (3,))
+        sq(1, (0,))
+        sq(1, (1,))
+        sq(1, (2,))
+        sqv(1, (3,))
         rn(1)
-        mn(1, (0,))
         tr("m", 0, 0, 2)
-        mnx(3, (2,))
-        mn(1, (1,))
-        tr("k", 0, 1, 1)
-        co("k", 0, 1, S)
-        sq(3, (0,))
-        sq(3, (1,))
-        rn(2)
-        mnx(3, (3,))
-        tr("m", 1, 0, 6)
         tr("m", 0, 1, 3)
+        mnx(3, (1,))
+        mnx(3, (2,))
+        mnx(3, (3,))
         co("m", 0, 0, S)
         co("m", 0, 1, S)
-        sq(3, (2,))
-        q1("k", 0)
-        sq(3, (3,))
-        rn(3)
+        q1("m", 0)
+        mn(1, (0,))
+        mn(1, (1,))
         mn(1, (2,))
         mn(1, (3,))
-        mn(2, (0,))
-        prepg("er", 0, 0)
-        prepg("ad", 0, 0)
-        prepg("ad", 0, 1)
-        q1("m", 0)
-        tr("k", 1, 0, 1)
+        sq(2, (0,))
+        sq(2, (1,))
+        sq(2, (2,))
+        sqv(2, (3,))
+        rn(2)
+        tr("m", 1, 0, 6)
         tr("m", 1, 1, 5)
+        co("m", 1, 0, S)
+        co("m", 1, 1, S)
+        q1("m", 1)
+        mn(2, (0,))
         mn(2, (1,))
         mn(2, (2,))
-        tr("m", 2, 0, 2)
         mn(2, (3,))
-        co("m", 1, 0, S)
-        prepg("er", 0, 3)
-        co("m", 1, 1, S)
-        mn(3, (0,))
-        mns(3, (1,))
-        co("m", 2, 0, S)
-        cl(0, 0)
-        rmax(0, 0)
+        sq(3, (0,))
+        sq(3, (1,))
+        sq(3, (2,))
+        sq(3, (3,))
+        rn(3)
+        tr("m", 2, 0, 2)
         tr("m", 2, 1, 3)
+        co("m", 2, 0, S)
         co("m", 2, 1, S)
         q1("m", 2)
-        tr("m", 3, 0, 6)
+        mn(3, (0,))
+        mns(3, (1,))
         mns(3, (2,))
         mns(3, (3,))
-        q1("m", 1)
-        tr("k", 1, 1, 5)
+        tr("m", 3, 0, 6)
         tr("m", 3, 1, 4)
         co("m", 3, 0, S)
         co("m", 3, 1, S)
-        cl(0, 2)
-        rmax(0, 2)
         q1("m", 3)
+        tr("k", 1, 0, 5)
+        tr("k", 1, 1, 7)
+        cl(0, 0)
+        rmax(0, 0)
         cl(0, 1)
         rmax(0, 1)
+        cl(0, 2)
+        rmax(0, 2)
         cl(0, 3)
-        prepg("er", 0, 1)
         rmax(0, 3)
-        co("k", 1, 0, S)
-        prepg("ad", 0, 2)
-        co("k", 1, 1, S)
-        cl(1, 1)
-        rmax(1, 1)
-        prepg("er", 0, 2)
-        cl(1, 2)
         nm(0)
-        rmax(1, 2)
+        co("k", 1, 0, S)
+        co("k", 1, 1, S)
+        q1("k", 1)
+        prepg("er", 0, 0)
+        prepg("er", 0, 1)
+        prepg("er", 0, 2)
+        prepg("er", 0, 3)
+        prepq("er", 0)
         ex1(0, 0)
-        ex1(0, 3)
-        cl(1, 3)
-        rmax(1, 3)
+        ex1(0, 1)
         ex1(0, 2)
+        ex1(0, 3)
         cl(1, 0)
         rmax(1, 0)
-        ex1(0, 1)
-        cl(2, 3)
-        prepq("er", 0)
-        prepg("ad", 0, 3)
-        prepg("er", 1, 0)
-        prepg("er", 1, 2)
+        cl(1, 1)
+        rmax(1, 1)
+        cl(1, 2)
+        rmax(1, 2)
+        cl(1, 3)
+        rmax(1, 3)
         nm(1)
-        ex1(1, 3)
-        rmax(2, 3)
-        ex1(1, 2)
-        cl(2, 0)
-        cl(2, 2)
-        rmax(2, 2)
-        rmax(2, 0)
+        ex1(1, 0)
         ex1(1, 1)
-        prepg("er", 1, 1)
+        ex1(1, 2)
+        ex1(1, 3)
+        prepg("ad", 0, 0)
+        prepg("ad", 0, 1)
+        prepg("ad", 0, 2)
+        prepg("ad", 0, 3)
+        prepq("ad", 0)
+        cl(2, 0)
+        rmax(2, 0)
         cl(2, 1)
         rmax(2, 1)
-        cl(3, 1)
-        ex1(1, 0)
-        prepq("ad", 0)
-        cl(3, 3)
-        prepg("ad", 1, 0)
-        prepg("ad", 1, 3)
-        cl(3, 0)
-        prepg("ad", 1, 2)
+        cl(2, 2)
+        rmax(2, 2)
+        cl(2, 3)
+        rmax(2, 3)
         nm(2)
-        rmax(3, 1)
+        ex1(2, 0)
         ex1(2, 1)
         ex1(2, 2)
-        ex1(2, 0)
         ex1(2, 3)
-        prepg("ad", 1, 1)
+        prepg("er", 1, 0)
+        prepg("er", 1, 1)
+        prepg("er", 1, 2)
+        prepg("er", 1, 3)
+        prepq("er", 1)
+        cl(3, 0)
+        rmax(3, 0)
+        cl(3, 1)
+        rmax(3, 1)
         cl(3, 2)
         rmax(3, 2)
+        cl(3, 3)
         rmax(3, 3)
-        rmax(3, 0)
         nm(3)
+        ex1(3, 0)
         ex1(3, 1)
         ex1(3, 2)
-        q1("k", 1)
+        ex1(3, 3)
+        prepg("ad", 1, 0)
+        prepg("ad", 1, 1)
+        prepg("ad", 1, 2)
+        prepg("ad", 1, 3)
         prepq("ad", 1)
         cl(4, 0)
         rmax(4, 0)
-        ex1(3, 0)
-        cl(5, 1)
+        cl(4, 1)
+        rmax(4, 1)
+        cl(4, 2)
+        rmax(4, 2)
         cl(4, 3)
         rmax(4, 3)
-        cl(4, 1)
-        cl(4, 2)
-        rmax(4, 1)
-        rmax(4, 2)
-        ex1(3, 3)
-        cf1(0)
         nm(4)
-        cl(5, 2)
         ex1(4, 0)
+        ex1(4, 1)
+        ex1(4, 2)
         ex1(4, 3)
-        rmax(5, 1)
+        cf1(0)
         cf2(0)
+        cf3(0)
         cl(5, 0)
         rmax(5, 0)
-        ex1(4, 2)
-        cf3(0)
-        wscale1(0, 0, 0)
-        wscale1(0, 0, 1)
+        cl(5, 1)
+        rmax(5, 1)
+        cl(5, 2)
+        rmax(5, 2)
         cl(5, 3)
         rmax(5, 3)
-        rmax(5, 2)
-        cl(6, 0)
-        ex1(4, 1)
-        cl(6, 2)
-        rmax(6, 0)
         nm(5)
-        prepg("er", 1, 3)
-        prepq("er", 1)
-        rmax(6, 2)
-        cl(6, 1)
-        ex1(5, 2)
-        rmax(6, 1)
         ex1(5, 0)
+        ex1(5, 1)
+        ex1(5, 2)
+        ex1(5, 3)
+        wscale1(0, 0, 0)
+        wscale1(0, 0, 1)
+        wscale1(0, 0, 2)
+        wscale1(0, 0, 3)
+        wil(0, 0)
+        wqz(0, 0)
+        cl(6, 0)
+        rmax(6, 0)
+        cl(6, 1)
+        rmax(6, 1)
+        cl(6, 2)
+        rmax(6, 2)
         cl(6, 3)
         rmax(6, 3)
-        wscale1(0, 0, 3)
-        wscale1(0, 0, 2)
-        ex1(5, 3)
-        ex1(5, 1)
-        wscale1(0, 1, 0)
-        wscale1(0, 1, 2)
-        cl(7, 2)
-        rmax(7, 2)
-        cl(7, 0)
-        rmax(7, 0)
-        wil(0, 0)
-        cl(7, 3)
-        rmax(7, 3)
-        wscale1(0, 1, 1)
-        wscale1(0, 1, 3)
-        cl(7, 1)
-        rmax(7, 1)
         nm(6)
         ex1(6, 0)
-        wqz(0, 0)
-        nm(7)
-        ex1(7, 3)
-        ex1(7, 0)
-        ex1(6, 2)
-        wil(0, 1)
-        wil(0, 2)
-        ex1(6, 3)
-        wil(0, 3)
         ex1(6, 1)
-        ex1(7, 2)
-        ex1(7, 1)
-        cf1(1)
+        ex1(6, 2)
+        ex1(6, 3)
+        wscale1(0, 1, 0)
+        wscale1(0, 1, 1)
+        wscale1(0, 1, 2)
+        wscale1(0, 1, 3)
+        wil(0, 1)
         wqz(0, 1)
+        cl(7, 0)
+        rmax(7, 0)
+        cl(7, 1)
+        rmax(7, 1)
+        cl(7, 2)
+        rmax(7, 2)
+        cl(7, 3)
+        rmax(7, 3)
+        nm(7)
+        ex1(7, 0)
+        ex1(7, 1)
+        ex1(7, 2)
+        ex1(7, 3)
+        wil(0, 2)
+        wqz(0, 2)
+        wilg(0, 3, 0)
+        wilg(0, 3, 1)
+        wilg(0, 3, 2)
+        wilg(0, 3, 3)
+        wqz(0, 3)
+        cf1(1)
         cf2(1)
         cf3(1)
+        wil(1, 0)
+        wqz(1, 0)
         wscale1(1, 1, 0)
         wscale1(1, 1, 1)
         wscale1(1, 1, 2)
         wscale1(1, 1, 3)
-        wscale1(1, 2, 0)
-        wscale1(1, 2, 2)
-        wqz(0, 2)
-        wscale1(1, 2, 3)
-        wil(1, 0)
         wil(1, 1)
-        wqz(1, 0)
-        mm2("er", 0)
-        mm2("ad", 1)
-        wscale1(1, 2, 1)
-        mm2("er", 2)
-        wscale1(1, 3, 0)
         wqz(1, 1)
-        mm2("er", 4)
-        wscale1(1, 3, 2)
-        wqz(0, 3)
+        mm2("er", 0)
+        wscale1(1, 2, 0)
+        wscale1(1, 2, 1)
+        wscale1(1, 2, 2)
+        wscale1(1, 2, 3)
         wil(1, 2)
         wqz(1, 2)
-        ea(0)
         mm2("er", 1)
-        ef(1)
         mm2("ad", 0)
-        mm2("er", 3)
-        mm2("er", 5)
-        mm2("ad", 2)
-        mm2("ad", 3)
-        em(1)
-        ea(2)
-        mm2("er", 6)
-        wscale1(1, 3, 3)
+        ea(0)
         eo(0)
-        mm2("ad", 4)
+        mm2("er", 2)
+        mm2("ad", 1)
+        ef(1)
+        em(1)
+        eo(1)
+        mm2("er", 3)
+        mm2("ad", 2)
+        ea(2)
+        eo(2)
+        mm2("er", 4)
+        mm2("ad", 3)
         ef(3)
         em(3)
-        eo(1)
-        wscale1(1, 3, 1)
-        ef(5)
-        eo(2)
-        mm2("ad", 6)
         eo(3)
-        mm2("ad", 7)
-        mm2("ad", 5)
-        mm2("er", 9)
         oi(0, 0, 512, S)
-        ea(4)
-        em(5)
-        ea(6)
-        mm2("er", 8)
-        wil(1, 3)
-        eo(4)
-        mm2("er", 7)
-        ef(7)
-        ef(9)
-        mm2("er", 10)
-        wqz(1, 3)
-        em(7)
-        mm2("er", 11)
         oq(0, 0, 512)
-        mm2("er", 13)
-        ef(11)
-        mm2("ad", 8)
+        wilg(1, 3, 0)
+        wilg(1, 3, 1)
+        wilg(1, 3, 2)
+        wilg(1, 3, 3)
+        wqz(1, 3)
+        mm2("er", 5)
+        mm2("ad", 4)
+        ea(4)
+        eo(4)
+        mm2("er", 6)
+        mm2("ad", 5)
+        ef(5)
+        em(5)
         eo(5)
-        mm2("ad", 9)
-        ef(13)
-        ea(8)
-        mm2("er", 12)
+        mm2("er", 7)
+        mm2("ad", 6)
+        ea(6)
         eo(6)
-        mm2("ad", 10)
+        mm2("er", 8)
+        mm2("ad", 7)
+        ef(7)
+        em(7)
         eo(7)
-        mm2("ad", 11)
-        em(9)
-        ea(10)
         oi(1, 0, 512, S)
+        oq(1, 0, 512)
+        mm2("er", 9)
+        mm2("ad", 8)
+        ea(8)
         eo(8)
-        mm2("ad", 12)
+        mm2("er", 10)
+        mm2("ad", 9)
+        ef(9)
+        em(9)
+        eo(9)
+        mm2("er", 11)
+        mm2("ad", 10)
+        ea(10)
         eo(10)
+        mm2("er", 12)
+        mm2("ad", 11)
+        ef(11)
         em(11)
         eo(11)
-        eo(9)
         oi(2, 0, 512, S)
-        mm2("er", 14)
-        mm2("ad", 14)
+        oq(2, 0, 512)
+        mm2("er", 13)
+        mm2("ad", 12)
         ea(12)
+        eo(12)
+        mm2("er", 14)
+        mm2("ad", 13)
+        ef(13)
         em(13)
+        eo(13)
+        mm2("er", 15)
+        mm2("ad", 14)
         ea(14)
         eo(14)
-        mm2("ad", 13)
-        mm2("er", 15)
-        ef(15)
-        oq(1, 0, 512)
-        oq(2, 0, 512)
-        eo(12)
-        eo(13)
         mm2("ad", 15)
+        ef(15)
         em(15)
         eo(15)
         oi(3, 0, 256, S)
-        oi(3, 256, 512, V)
         oq(3, 0, 256)
+        oi(3, 256, 512, V)
         oq(3, 256, 512)

@@ -4,8 +4,14 @@ import concourse.mybir as mybir
 from concourse.masks import make_identity
 
 T, N, W = 1024, 2048, 512
-P, J, G = 128, 4, 512
+P = 128
+J = 4
+G = P * J
 TG, NG = T // G, N // G
+TILES = TG * J
+HALF = W // 2
+RUN = 4
+PIECE = 128
 FLOPS = 3 * 2 * T * N * W
 
 F32 = mybir.dt.float32
@@ -16,663 +22,503 @@ U8 = mybir.dt.uint8
 FP8X4 = mybir.dt.float8_e4m3fn_x4
 ALU = mybir.AluOpType
 ACT = mybir.ActivationFunctionType
-AX = mybir.AxisListType
+X = mybir.AxisListType.X
+
+
+def row_tiles(x, g):
+    return x.rearrange("(g p t) w -> g p t w", p=P, t=J)[g]
+
+
+def by_runs(x):
+    return x.rearrange("p t (c i) -> p c t i", i=RUN)
+
+
+def into_words(x):
+    return x.rearrange("p (c i) t -> p c t i", i=RUN)
 
 
 def tile_ntmcontentaddresseraseadd_x1_kernel(tc, key, mem, gm, s, erase, add, out_0, out_1, out_2):
     nc = tc.nc
-    V, S, GP, PE = nc.vector, nc.scalar, nc.gpsimd, nc.tensor
     with ExitStack() as ctx:
         keep = ctx.enter_context(tc.tile_pool(name="keep", bufs=1))
         work = ctx.enter_context(tc.tile_pool(name="work", bufs=2))
         psum = ctx.enter_context(tc.psum_pool(name="psum", bufs=1))
+        ctx.enter_context(tc.manual_schedule())
 
-        def rows(x, g):
-            return x.rearrange("(g p t) w -> g p t w", p=P, t=J)[g]
+        def kept(name, shape, dtype):
+            return keep.tile(shape, dtype, name=name, tag=name, align_bytes=64)
 
-        def keep_tile(name, shape, dt):
-            return keep.tile(shape, dt, name=name, tag=name, align_bytes=64)
+        def passing(name, shape, dtype, bufs):
+            return work.tile(shape, dtype, name=name, tag=name, bufs=bufs, align_bytes=64)
 
         def bank(k, name):
-            return psum.tile([P, 512], F32, name=name, tag="b%d" % k)
+            return psum.tile([P, 512], F32, name=name, tag="bank%d" % k)
 
-        mem_sb = [keep_tile("mem%d" % g, [P, J, W], BF16) for g in range(NG)]
-        key_sb = [keep_tile("key%d" % g, [P, J, W], BF16) for g in range(TG)]
-        ea_sb = {}
-        for x in ("er", "ad"):
-            for g in range(TG):
-                ea_sb[x, g] = keep_tile("%s%d" % (x, g), [P, J, W], BF16)
-        gm_row = keep_tile("gm_row", [P, W], BF16)
-        ones = keep_tile("ones", [P, P], BF16)
-        ones_in = keep_tile("ones_in", [P, P], BF16)
-        s_sb = keep_tile("s_sb", [P, TG, J], BF16)
-        ident = keep_tile("ident", [P, P], F32)
-        gm_b = keep_tile("gm_b", [P, W], F32)
-        ssq = keep_tile("ssq", [P, NG, J], F32)
-        rinv = keep_tile("rinv", [P, NG, J], F32)
-        mq = keep_tile("mq", [P, NG, G], U32)
-        ms = keep_tile("ms", [P, NG, G], U8)
-        kq = keep_tile("kq", [P, TG, G], U32)
-        ks = keep_tile("ks", [P, TG, G], U8)
-        wq = [keep_tile("wq%d" % g, [P, N], U32) for g in range(TG)]
-        wsc = [keep_tile("wsc%d" % g, [P, N], U8) for g in range(TG)]
-        eq = {}
-        es = {}
-        for x in ("er", "ad"):
-            for g in range(TG):
-                eq[x, g] = keep_tile("q%s%d" % (x, g), [P, W], U32)
-                es[x, g] = keep_tile("s%s%d" % (x, g), [P, W], U8)
-        e_sb = [keep_tile("e%d" % g, [P, J, N], F32) for g in range(TG)]
-        mx = keep_tile("mx", [P, TG * J, NG], F32)
-        nmax = keep_tile("nmax", [P, TG * J], F32)
-        sums = keep_tile("sums", [P, TG * J, NG], F32)
-        tot = keep_tile("tot", [P, TG, J], F32)
-        rtot = keep_tile("rtot", [P, TG, J], F32)
-        coef = keep_tile("coef", [P, TG, J], F32)
+        mem_rows = [kept("mem%d" % g, [P, J, W], BF16) for g in range(NG)]
+        key_rows = [kept("key%d" % g, [P, J, W], BF16) for g in range(TG)]
+        write_keys = [(what, g) for g in range(TG) for what in ("erase", "add")]
+        write_rows = {k: kept("%s%d" % k, [P, J, W], BF16) for k in write_keys}
+        gain_row = kept("gain_row", [P, W], BF16)
+        gain = kept("gain", [P, W], F32)
+        ones_in = kept("ones_in", [P, P], BF16)
+        ones = kept("ones", [P, P], BF16)
+        identity = kept("identity", [P, P], F32)
+        strength = kept("strength", [P, TG, J], BF16)
+        squares = kept("squares", [P, NG, J], F32)
+        inverse = kept("inverse", [P, NG, J], F32)
+        row_max = kept("row_max", [P, TILES, NG], F32)
+        minus_max = kept("minus_max", [P, TILES], F32)
+        sums = kept("sums", [P, TILES, NG], F32)
+        total = kept("total", [P, TG, J], F32)
+        inverse_total = kept("inverse_total", [P, TG, J], F32)
+        factor = kept("factor", [P, TG, J], F32)
 
-        V.memset(gm_row[:], 0.0)
-        V.memset(ones_in[:], 1.0)
-        S.activation(out=ones[:], in_=ones_in[:], func=ACT.Abs_reciprocal_sqrt)
-        make_identity(nc, ident[:])
-        nc.sync.dma_start(out=mem_sb[0][:, 0:2, :], in_=rows(mem, 0)[:, 0:2, :])
-        nc.sync.dma_start(out=gm_row[0:1, :], in_=gm.rearrange("(o w) -> o w", o=1))
-        nc.sync.dma_start(out=mem_sb[0][:, 2:4, :], in_=rows(mem, 0)[:, 2:4, :])
-        nc.sync.dma_start(out=key_sb[0][:], in_=rows(key, 0))
-        nc.sync.dma_start(out=mem_sb[1][:], in_=rows(mem, 1))
-        nc.sync.dma_start(out=mem_sb[2][:], in_=rows(mem, 2))
-        nc.sync.dma_start(out=mem_sb[3][:], in_=rows(mem, 3))
-        nc.sync.dma_start(out=key_sb[1][:], in_=rows(key, 1))
-        nc.sync.dma_start(out=s_sb[:], in_=s.rearrange("(g p t) -> p g t", p=P, t=J))
+        mem_q = kept("mem_q", [P, NG, G], U32), kept("mem_s", [P, NG, G], U8)
+        key_q = kept("key_q", [P, TG, G], U32), kept("key_s", [P, TG, G], U8)
+        w_q = [kept("w_q%d" % g, [P, N], U32) for g in range(TG)]
+        w_s = [kept("w_s%d" % g, [P, N], U8) for g in range(TG)]
+        write_q = {k: kept("%s_q%d" % k, [P, W], U32) for k in write_keys}
+        write_s = {k: kept("%s_s%d" % k, [P, W], U8) for k in write_keys}
+        exps = [kept("exps0", [P, J, N], F32), kept("exps1", [P, J, N], F32)]
+
+        nc.vector.memset(gain_row[:], 0.0)
+        nc.vector.memset(ones_in[:], 1.0)
+        make_identity(nc, identity[:])
+        nc.sync.dma_start(out=mem_rows[0][:, 0:2, :], in_=row_tiles(mem, 0)[:, 0:2, :])
+        nc.sync.dma_start(out=gain_row[0:1, :], in_=gm.rearrange("(o w) -> o w", o=1))
+        nc.sync.dma_start(out=mem_rows[0][:, 2:4, :], in_=row_tiles(mem, 0)[:, 2:4, :])
+        nc.sync.dma_start(out=key_rows[0][:], in_=row_tiles(key, 0))
+        for g in range(1, NG):
+            nc.sync.dma_start(out=mem_rows[g][:], in_=row_tiles(mem, g))
+        nc.sync.dma_start(out=key_rows[1][:], in_=row_tiles(key, 1))
+        nc.sync.dma_start(out=strength[:], in_=s.rearrange("(g p t) -> p g t", p=P, t=J))
         for g in range(TG):
-            nc.sync.dma_start(out=ea_sb["er", g][:], in_=rows(erase, g))
-            nc.sync.dma_start(out=ea_sb["ad", g][:], in_=rows(add, g))
+            nc.sync.dma_start(out=write_rows["erase", g][:], in_=row_tiles(erase, g))
+            nc.sync.dma_start(out=write_rows["add", g][:], in_=row_tiles(add, g))
+        nc.scalar.activation(out=ones[:], in_=ones_in[:], func=ACT.Abs_reciprocal_sqrt)
 
-        trb = {}
+        gain_bank, scaled_rows, normed, turned, words, logit_bank = {}, {}, {}, {}, {}, {}
+        writes, w_rows, w_words, product_bank, kept_part, left_factor = {}, {}, {}, {}, {}, {}
+        result, result_words, planes = {}, {}, {}
 
-        def gm_bcast():
-            b = bank(7, "gmps")
-            PE.matmul(b[:], lhsT=ones[:], rhs=gm_row[:], start=True, stop=True)
-            trb["gm"] = b
+        def spread_gain():
+            gain_bank[0] = bank(7, "gain_bank")
+            nc.tensor.matmul(gain_bank[0][:], lhsT=ones[:], rhs=gain_row[:], start=True, stop=True)
 
-        def gm_copy():
-            S.copy(gm_b[:], trb["gm"][:])
+        def keep_gain():
+            nc.scalar.copy(gain[:], gain_bank[0][:])
 
-        def sq(g, ts):
-            for t in ts:
-                junk = work.tile([P, W], BF16, name="junk", tag="junk")
-                S.activation(out=junk[:], in_=mem_sb[g][:, t, :], func=ACT.Square, accum_out=ssq[:, g, t : t + 1])
+        def square_on_scalar(g, t):
+            unused = passing("squared_s", [P, W], BF16, 2)
+            nc.scalar.activation(
+                out=unused[:], in_=mem_rows[g][:, t, :], func=ACT.Square, accum_out=squares[:, g, t : t + 1]
+            )
 
-        def sqv(g, ts):
-            for t in ts:
-                junk = work.tile([P, W], BF16, name="junkv", tag="junkv")
-                V.scalar_tensor_tensor(out=junk[:], in0=mem_sb[g][:, t, :], scalar=1.0, in1=mem_sb[g][:, t, :], op0=ALU.mult, op1=ALU.mult, accum_out=ssq[:, g, t : t + 1])
+        def square_on_vector(g, t):
+            unused = passing("squared_v", [P, W], BF16, 2)
+            x = mem_rows[g][:, t, :]
+            nc.vector.scalar_tensor_tensor(
+                out=unused[:], in0=x, scalar=1.0, in1=x, op0=ALU.mult, op1=ALU.mult, accum_out=squares[:, g, t : t + 1]
+            )
 
-        def rn(g):
-            S.activation(out=rinv[:, g, :], in_=ssq[:, g, :], func=ACT.Abs_reciprocal_sqrt, bias=1e-6)
+        def inverse_length(g):
+            nc.scalar.activation(out=inverse[:, g, :], in_=squares[:, g, :], func=ACT.Abs_reciprocal_sqrt, bias=1e-6)
 
-        mnr = {}
+        def norm_on_vector(g, t):
+            normed[g, t] = passing("normed_v", [P, W], BF16, 4)
+            nc.vector.scalar_tensor_tensor(
+                out=normed[g, t][:],
+                in0=mem_rows[g][:, t, :],
+                scalar=inverse[:, g, t : t + 1],
+                in1=gain_bank[0][:],
+                op0=ALU.mult,
+                op1=ALU.mult,
+            )
 
-        def mn(g, ts):
-            for t in ts:
-                m = work.tile([P, W], BF16, name="mnr", tag="mnr", bufs=6)
-                V.scalar_tensor_tensor(out=m[:], in0=mem_sb[g][:, t, :], scalar=rinv[:, g, t : t + 1], in1=trb["gm"][:], op0=ALU.mult, op1=ALU.mult)
-                mnr[g, t] = m
+        def gain_on_gpsimd(g, t):
+            scaled_rows[g, t] = passing("scaled_row", [P, W], F32, 4)
+            nc.gpsimd.tensor_tensor(out=scaled_rows[g, t][:], in0=mem_rows[g][:, t, :], in1=gain[:], op=ALU.mult)
 
-        xg = {}
+        def norm_on_scalar(g, t):
+            normed[g, t] = passing("normed_s", [P, W], BF16, 3)
+            nc.scalar.activation(
+                out=normed[g, t][:], in_=scaled_rows[g, t][:], func=ACT.Copy, scale=inverse[:, g, t : t + 1]
+            )
 
-        def mnx(g, ts):
-            for t in ts:
-                x = work.tile([P, W], F32, name="xg", tag="xg", bufs=4)
-                GP.tensor_tensor(out=x[:], in0=mem_sb[g][:, t, :], in1=gm_b[:], op=ALU.mult)
-                xg[g, t] = x
-
-        def mns(g, ts):
-            for t in ts:
-                m = work.tile([P, W], BF16, name="mnr", tag="mnr", bufs=6)
-                S.activation(out=m[:], in_=xg[g, t][:], func=ACT.Copy, scale=rinv[:, g, t : t + 1])
-                mnr[g, t] = m
-
-        def tr(what, g, h, bk):
-            b = bank(bk, "tr")
-            v = b[:].rearrange("p (i u r) -> p i u r", i=2, u=2)
+        def turn(what, g, h, k):
+            turned[what, g, h] = bank(k, "turned")
+            view = turned[what, g, h][:].rearrange("p (i u r) -> p i u r", i=2, u=2)
             for i in range(2):
                 t = 2 * h + i
-                src = mnr[g, t][:] if what == "m" else key_sb[g][:, t, :]
-                words = src.bitcast(F32)
+                rows = key_rows[g][:, t, :] if what == "key" else normed[g, t][:]
                 for u in range(2):
-                    PE.transpose(v[:, i, u, :], words[:, u::2], ident[:])
-            trb[what, g, h] = b
+                    nc.tensor.transpose(view[:, i, u, :], rows.bitcast(F32)[:, u::2], identity[:])
 
-        grp = {}
+        def unload(what, g, h):
+            if h == 0:
+                words[what, g] = passing("words", [P, G, J], BF16, 3)
+            pairs = words[what, g][:].rearrange("p n j -> p (n j)").bitcast(F32)[:, h * 512 : (h + 1) * 512]
+            nc.scalar.copy(
+                pairs.rearrange("p (i r u) -> p i r u", i=2, u=2),
+                turned[what, g, h][:].rearrange("p (i u r) -> p i r u", i=2, u=2),
+            )
 
-        def co(what, g, h, eng):
-            if (what, g) not in grp:
-                grp[what, g] = work.tile([P, G, J], BF16, name="grp", tag="grp", bufs=3, align_bytes=64)
-            dst = grp[what, g][:].rearrange("p n j -> p (n j)").bitcast(F32)[:, h * 512 : h * 512 + 512]
-            dst = dst.rearrange("p (i r u) -> p i r u", i=2, u=2)
-            src = trb[what, g, h][:].rearrange("p (i u r) -> p i r u", i=2, u=2)
-            if eng is V:
-                V.tensor_copy(out=dst, in_=src)
-            else:
-                S.copy(dst, src)
+        def quantize_rows(what, g):
+            codes, scales = key_q if what == "key" else mem_q
+            nc.vector.quantize_mx(
+                out=codes[:, g, :].bitcast(FP8X4),
+                scales=scales[:, g, :],
+                in_=words[what, g][:].rearrange("p n j -> p (n j)"),
+            )
 
-        def q1(what, g):
-            c, sc = (mq, ms) if what == "m" else (kq, ks)
-            V.quantize_mx(out=c[:, g, :].bitcast(FP8X4), scales=sc[:, g, :], in_=grp[what, g][:].rearrange("p n j -> p (n j)"))
-
-        clb = {}
-
-        def cl(i, c):
-            b = bank((i % 2) * 4 + c, "cl")
+        def logits(i, c):
             tg, t = divmod(i, J)
-            PE.matmul_mx(
-                out=b[:],
-                lhsT=kq[:, tg, t * P : t * P + P].bitcast(FP8X4),
-                lhsT_scale=ks[:, tg, t * P : t * P + P],
-                rhs=mq[:, c, :].bitcast(FP8X4),
-                rhs_scale=ms[:, c, :],
+            cols = slice(t * P, (t + 1) * P)
+            logit_bank[i, c] = bank(i % 2 * NG + c, "logits")
+            nc.tensor.matmul_mx(
+                out=logit_bank[i, c][:],
+                lhsT=key_q[0][:, tg, cols].bitcast(FP8X4),
+                lhsT_scale=key_q[1][:, tg, cols],
+                rhs=mem_q[0][:, c, :].bitcast(FP8X4),
+                rhs_scale=mem_q[1][:, c, :],
                 start=True,
                 stop=True,
             )
-            clb[i, c] = b
 
-        def rmax(i, c):
-            V.tensor_reduce(out=mx[:, i, c : c + 1], in_=clb[i, c][:], axis=AX.X, op=ALU.max)
+        def largest(i, c):
+            nc.vector.tensor_reduce(out=row_max[:, i, c : c + 1], in_=logit_bank[i, c][:], axis=X, op=ALU.max)
 
-        def nm(i):
-            V.tensor_reduce(out=nmax[:, i : i + 1], in_=mx[:, i, :], axis=AX.X, op=ALU.max, negate=True)
-
-        def ex(i, cs=range(NG)):
+        def exponentials(i):
             tg, t = divmod(i, J)
-            for c in cs:
-                S.activation(out=e_sb[tg][:, t, c * G : c * G + G], in_=clb[i, c][:], func=ACT.Exp, bias=nmax[:, i : i + 1], accum_out=sums[:, i, c : c + 1])
+            nc.vector.tensor_reduce(out=minus_max[:, i : i + 1], in_=row_max[:, i, :], axis=X, op=ALU.max, negate=True)
+            for c in range(NG):
+                nc.scalar.activation(
+                    out=exps[tg][:, t, c * G : (c + 1) * G],
+                    in_=logit_bank[i, c][:],
+                    func=ACT.Exp,
+                    bias=minus_max[:, i : i + 1],
+                    accum_out=sums[:, i, c : c + 1],
+                )
 
-        eag = {}
+        def row_sums(tg):
+            nc.vector.tensor_reduce(out=total[:, tg, :], in_=sums[:, tg * J : (tg + 1) * J, :], axis=X, op=ALU.add)
 
-        def prepg(x, g, k):
-            if (x, g) not in eag:
-                eag[x, g] = work.tile([P, W, J], BF16, name="eag", tag="eag", bufs=2, align_bytes=64)
-            c = slice(128 * k, 128 * k + 128)
-            GP.tensor_scalar(out=eag[x, g][:, c, :], in0=ea_sb[x, g][:, :, c].rearrange("p t w -> p w t"), scalar1=1.0, scalar2=0.0, op0=ALU.mult, op1=ALU.add)
+        def invert_sums(tg):
+            nc.vector.reciprocal(inverse_total[:, tg, :], total[:, tg, :])
 
-        def prep(x, g, eng):
-            d = work.tile([P, W, J], BF16, name="eag", tag="eag", bufs=2, align_bytes=64)
-            src = ea_sb[x, g][:].rearrange("p t w -> p w t")
-            if eng is V:
-                V.tensor_copy(out=d[:], in_=src)
-            elif eng is S:
-                S.copy(d[:], src)
-            else:
-                for w0 in range(0, W, 128):
-                    GP.tensor_scalar(out=d[:, w0 : w0 + 128, :], in0=src[:, w0 : w0 + 128, :], scalar1=1.0, scalar2=0.0, op0=ALU.mult, op1=ALU.add)
-            eag[x, g] = d
+        def row_factors(tg):
+            nc.vector.scalar_tensor_tensor(
+                out=factor[:, tg, :],
+                in0=strength[:, tg, :],
+                scalar=64.0,
+                in1=inverse_total[:, tg, :],
+                op0=ALU.mult,
+                op1=ALU.mult,
+            )
 
-        def prepq(x, g):
-            V.quantize_mx(out=eq[x, g][:].bitcast(FP8X4), scales=es[x, g][:], in_=eag[x, g][:].rearrange("p w t -> p (w t)"))
-
-        def cf1(tg):
-            V.tensor_reduce(out=tot[:, tg, :], in_=sums[:, tg * J : tg * J + J, :], axis=AX.X, op=ALU.add)
-
-        def cf2(tg):
-            V.reciprocal(rtot[:, tg, :], tot[:, tg, :])
-
-        def cf3(tg):
-            V.scalar_tensor_tensor(out=coef[:, tg, :], in0=s_sb[:, tg, :], scalar=64.0, in1=rtot[:, tg, :], op0=ALU.mult, op1=ALU.mult)
-
-        def cf(tg):
-            V.tensor_reduce(out=tot[:, tg, :], in_=sums[:, tg * J : tg * J + J, :], axis=AX.X, op=ALU.add)
-            V.reciprocal(rtot[:, tg, :], tot[:, tg, :])
-            V.scalar_tensor_tensor(out=coef[:, tg, :], in0=s_sb[:, tg, :], scalar=64.0, in1=rtot[:, tg, :], op0=ALU.mult, op1=ALU.mult)
-
-        wsb = {}
-        w16 = {}
-
-        def wscale(tg, c):
-            d = work.tile([P, J, G], BF16, name="wsb", tag="wsb", bufs=2, align_bytes=64)
+        def scale_rows(tg, c):
+            w_rows[tg, c] = passing("w_rows", [P, J, G], BF16, 2)
             for t in range(J):
-                S.activation(out=d[:, t, :], in_=e_sb[tg][:, t, c * G : c * G + G], func=ACT.Copy, scale=coef[:, tg, t : t + 1])
-            wsb[tg, c] = d
+                nc.scalar.activation(
+                    out=w_rows[tg, c][:, t, :],
+                    in_=exps[tg][:, t, c * G : (c + 1) * G],
+                    func=ACT.Copy,
+                    scale=factor[:, tg, t : t + 1],
+                )
 
-        def wil(tg, c, eng=V):
-            d = work.tile([P, G, J], BF16, name="w16", tag="w16", bufs=3, align_bytes=64)
-            if (tg, c) in wsb:
-                V.tensor_copy(out=d[:], in_=wsb[tg, c][:].rearrange("p t n -> p n t"))
-            else:
-                step = G if eng is V else 128
-                for n0 in range(0, G, step):
-                    eng.tensor_tensor(
-                        out=d[:, n0 : n0 + step, :],
-                        in0=e_sb[tg][:, :, c * G + n0 : c * G + n0 + step].rearrange("p t n -> p n t"),
-                        in1=coef[:, tg, :].unsqueeze(1).to_broadcast([P, step, J]),
-                        op=ALU.mult,
-                    )
-            w16[tg, c] = d
+        def interleave(tg, c):
+            w_words[tg, c] = passing("w_words", [P, G, J], BF16, 2)
+            nc.vector.tensor_copy(out=into_words(w_words[tg, c][:]), in_=by_runs(w_rows[tg, c][:]))
 
-        def wilg(tg, c, k):
-            if (tg, c) not in w16:
-                w16[tg, c] = work.tile([P, G, J], BF16, name="w16", tag="w16", bufs=3, align_bytes=64)
-            n0 = 128 * k
-            GP.tensor_tensor(
-                out=w16[tg, c][:, n0 : n0 + 128, :],
-                in0=e_sb[tg][:, :, c * G + n0 : c * G + n0 + 128].rearrange("p t n -> p n t"),
-                in1=coef[:, tg, :].unsqueeze(1).to_broadcast([P, 128, J]),
+        def scale_and_interleave(tg, c):
+            w_words[tg, c] = passing("w_words", [P, G, J], BF16, 2)
+            nc.vector.tensor_tensor(
+                out=w_words[tg, c][:],
+                in0=exps[tg][:, :, c * G : (c + 1) * G].rearrange("p t n -> p n t"),
+                in1=factor[:, tg, :].unsqueeze(1).to_broadcast([P, G, J]),
                 op=ALU.mult,
             )
 
-        def wscale1(tg, c, t):
-            if (tg, c) not in wsb:
-                wsb[tg, c] = work.tile([P, J, G], BF16, name="wsb", tag="wsb", bufs=2, align_bytes=64)
-            S.activation(out=wsb[tg, c][:, t, :], in_=e_sb[tg][:, t, c * G : c * G + G], func=ACT.Copy, scale=coef[:, tg, t : t + 1])
+        def scale_and_interleave_piece(tg, c, k):
+            if k == 0:
+                w_words[tg, c] = passing("w_words_g", [P, G, J], BF16, 1)
+            cols = slice(k * PIECE, (k + 1) * PIECE)
+            from_cols = slice(c * G + k * PIECE, c * G + (k + 1) * PIECE)
+            nc.gpsimd.tensor_tensor(
+                out=w_words[tg, c][:, cols, :],
+                in0=exps[tg][:, :, from_cols].rearrange("p t n -> p n t"),
+                in1=factor[:, tg, :].unsqueeze(1).to_broadcast([P, PIECE, J]),
+                op=ALU.mult,
+            )
 
-        def ex1(i, c):
-            tg, t = divmod(i, J)
-            S.activation(out=e_sb[tg][:, t, c * G : c * G + G], in_=clb[i, c][:], func=ACT.Exp, bias=nmax[:, i : i + 1], accum_out=sums[:, i, c : c + 1])
+        def quantize_w(tg, c):
+            cols = slice(c * G, (c + 1) * G)
+            nc.vector.quantize_mx(
+                out=w_q[tg][:, cols].bitcast(FP8X4),
+                scales=w_s[tg][:, cols],
+                in_=w_words[tg, c][:].rearrange("p n t -> p (n t)"),
+            )
 
-        def wqz(tg, c):
-            cols = slice(c * G, c * G + G)
-            V.quantize_mx(out=wq[tg][:, cols].bitcast(FP8X4), scales=wsc[tg][:, cols], in_=w16[tg, c][:].rearrange("p n t -> p (n t)"))
+        def interleave_write(what, g):
+            writes[what, g] = passing("write_words", [P, W, J], BF16, 2)
+            for k in range(W // PIECE):
+                cols = slice(k * PIECE, (k + 1) * PIECE)
+                nc.gpsimd.tensor_scalar(
+                    out=writes[what, g][:, cols, :],
+                    in0=write_rows[what, g][:, :, cols].rearrange("p t w -> p w t"),
+                    scalar1=1.0,
+                    scalar2=0.0,
+                    op0=ALU.mult,
+                    op1=ALU.add,
+                )
 
-        eb = {}
-        o32 = {}
+        def quantize_write(what, g):
+            nc.vector.quantize_mx(
+                out=write_q[what, g][:].bitcast(FP8X4),
+                scales=write_s[what, g][:],
+                in_=writes[what, g][:].rearrange("p w t -> p (w t)"),
+            )
 
-        pos = []
-
-        def mm2(x, j):
-            g, t = divmod(j, J)
-            cols = slice(g * G + t * P, g * G + t * P + P)
-            b = bank(len(pos) % 8, "mm2")
-            pos.append(1)
+        def product(what, j):
+            cols = slice(j * P, (j + 1) * P)
+            product_bank[what, j] = bank((2 * j + (7 if what == "erase" else 2)) % 8, what)
             for tg in range(TG):
-                PE.matmul_mx(
-                    out=b[:],
-                    lhsT=wq[tg][:, cols].bitcast(FP8X4),
-                    lhsT_scale=wsc[tg][:, cols],
-                    rhs=eq[x, tg][:].bitcast(FP8X4),
-                    rhs_scale=es[x, tg][:],
+                nc.tensor.matmul_mx(
+                    out=product_bank[what, j][:],
+                    lhsT=w_q[tg][:, cols].bitcast(FP8X4),
+                    lhsT_scale=w_s[tg][:, cols],
+                    rhs=write_q[what, tg][:].bitcast(FP8X4),
+                    rhs_scale=write_s[what, tg][:],
                     start=(tg == 0),
                     stop=(tg == TG - 1),
                 )
-            eb[x, j] = b
 
-        ab = {}
-        fb = {}
-        done = {}
-
-        def ea(j):
+        def keep_on_vector(j):
             g, t = divmod(j, J)
-            a = work.tile([P, W], F32, name="a", tag="a", bufs=4)
-            V.scalar_tensor_tensor(out=a[:], in0=eb["er", j][:], scalar=1.0, in1=mem_sb[g][:, t, :], op0=ALU.subtract, op1=ALU.mult)
-            ab[j] = (a, ALU.subtract)
+            kept_part[j] = passing("kept_v", [P, W], F32, 3), ALU.subtract
+            nc.vector.scalar_tensor_tensor(
+                out=kept_part[j][0][:],
+                in0=product_bank["erase", j][:],
+                scalar=1.0,
+                in1=mem_rows[g][:, t, :],
+                op0=ALU.subtract,
+                op1=ALU.mult,
+            )
 
-        def ef(j):
+        def left_on_scalar(j):
+            left_factor[j] = passing("left_factor", [P, W], F32, 2)
+            nc.scalar.activation(
+                out=left_factor[j][:], in_=product_bank["erase", j][:], func=ACT.Copy, scale=-1.0, bias=1.0
+            )
+
+        def keep_on_gpsimd(j):
             g, t = divmod(j, J)
-            f = work.tile([P, W], F32, name="f", tag="f", bufs=2)
-            S.activation(out=f[:], in_=eb["er", j][:], func=ACT.Copy, scale=-1.0, bias=1.0)
-            fb[j] = f
+            kept_part[j] = passing("kept_g", [P, W], F32, 2), ALU.add
+            nc.gpsimd.tensor_tensor(
+                out=kept_part[j][0][:], in0=left_factor[j][:], in1=mem_rows[g][:, t, :], op=ALU.mult
+            )
 
-        def em(j):
+        def finish(j):
             g, t = divmod(j, J)
-            f = fb[j]
-            a = work.tile([P, W], F32, name="a", tag="a", bufs=4)
-            GP.tensor_tensor(out=a[:], in0=f[:], in1=mem_sb[g][:, t, :], op=ALU.mult)
-            ab[j] = (a, ALU.add)
+            if j == 0:
+                space = keep.tile([P, NG, J, W], F32, name="result", tag="exps0", align_bytes=64)
+                for n in range(NG):
+                    result[n] = space[:, n, :, :]
+            part, op = kept_part[j]
+            nc.vector.tensor_tensor(out=result[g][:, t, :], in0=product_bank["add", j][:], in1=part[:], op=op)
+            if t % 2 == 1:
+                nc.sync.dma_start(out=row_tiles(out_0, g)[:, t - 1 : t + 1, :], in_=result[g][:, t - 1 : t + 1, :])
 
-        def eo(j):
-            g, t = divmod(j, J)
-            if 0 not in o32:
-                o_all = keep.tile([P, NG, J, W], F32, name="o32", tag="e0", align_bytes=64)
-                for gg in range(NG):
-                    o32[gg] = o_all[:, gg, :, :]
-            a, op = ab[j]
-            V.tensor_tensor(out=o32[g][:, t, :], in0=eb["ad", j][:], in1=a[:], op=op)
-            done[j] = True
-            if (j ^ 1) in done:
-                t |= 1
-                nc.sync.dma_start(out=rows(out_0, g)[:, t - 1 : t + 1, :], in_=o32[g][:, t - 1 : t + 1, :])
+        def round_on_scalar(g, h):
+            result_words[g, h] = passing("result_s", [P, HALF, J], BF16, 2)
+            nc.scalar.copy(
+                into_words(result_words[g, h][:]), by_runs(result[g][:, :, h * HALF : (h + 1) * HALF])
+            )
 
-        o16 = {}
-        oc = {}
-        left = {}
+        def round_on_vector(g, h):
+            result_words[g, h] = passing("result_v", [P, HALF, J], BF16, 1)
+            nc.vector.tensor_copy(
+                out=into_words(result_words[g, h][:]), in_=by_runs(result[g][:, :, h * HALF : (h + 1) * HALF])
+            )
 
-        def oi(g, c0, c1, eng):
-            d = work.tile([P, c1 - c0, J], BF16, name="o16", tag="o16", bufs=2, align_bytes=64)
-            src = o32[g][:, :, c0:c1].rearrange("p t w -> p w t")
-            if eng is V:
-                V.tensor_copy(out=d[:], in_=src)
-            else:
-                S.copy(d[:], src)
-            o16[g, c0] = d
+        def quantize_result(g, h):
+            if g not in planes:
+                planes[g] = passing("out_q", [P, W], U32, 2), passing("out_s", [P, W], U8, 2)
+            codes, scales = planes[g]
+            cols = slice(h * HALF, (h + 1) * HALF)
+            nc.vector.quantize_mx(
+                out=codes[:, cols].bitcast(FP8X4),
+                scales=scales[:, cols],
+                in_=result_words[g, h][:].rearrange("p w t -> p (w t)"),
+            )
 
-        def oq(g, c0, c1):
-            if g not in oc:
-                oc[g] = (work.tile([P, W], U32, name="oc", tag="oc", align_bytes=64), work.tile([P, W], U8, name="os", tag="os", align_bytes=64))
-                left[g] = W
-            c, sc = oc[g]
-            V.quantize_mx(out=c[:, c0:c1].bitcast(FP8X4), scales=sc[:, c0:c1], in_=o16[g, c0][:].rearrange("p w t -> p (w t)"))
-            left[g] -= c1 - c0
-            if left[g] == 0:
-                nc.sync.dma_start(out=out_1[g].rearrange("p m t -> p (m t)").bitcast(I32), in_=c[:].bitcast(I32))
-                for q in range(4):
-                    nc.sync.dma_start(out=out_2[g, 4 * q : 4 * q + 4, :].bitcast(I32), in_=sc[32 * q : 32 * q + 4, :].bitcast(I32))
+        def store_planes(g):
+            codes, scales = planes[g]
+            nc.sync.dma_start(out=out_1[g].rearrange("p m t -> p (m t)").bitcast(I32), in_=codes[:].bitcast(I32))
+            for q in range(4):
+                nc.sync.dma_start(
+                    out=out_2[g, 4 * q : 4 * q + 4, :].bitcast(I32), in_=scales[32 * q : 32 * q + 4, :].bitcast(I32)
+                )
 
-        gm_bcast()
-        sq(0, (0,))
-        sq(0, (1,))
-        sqv(0, (2,))
-        sqv(0, (3,))
-        rn(0)
-        gm_copy()
-        tr("k", 0, 0, 0)
-        tr("k", 0, 1, 1)
-        co("k", 0, 0, S)
-        co("k", 0, 1, S)
-        q1("k", 0)
-        mn(0, (0,))
-        mn(0, (1,))
-        mn(0, (2,))
-        mn(0, (3,))
-        sq(1, (0,))
-        sq(1, (1,))
-        sq(1, (2,))
-        sqv(1, (3,))
-        rn(1)
-        tr("m", 0, 0, 2)
-        tr("m", 0, 1, 3)
-        mnx(3, (1,))
-        mnx(3, (2,))
-        mnx(3, (3,))
-        co("m", 0, 0, S)
-        co("m", 0, 1, S)
-        q1("m", 0)
-        mn(1, (0,))
-        mn(1, (1,))
-        mn(1, (2,))
-        mn(1, (3,))
-        sq(2, (0,))
-        sq(2, (1,))
-        sq(2, (2,))
-        sqv(2, (3,))
-        rn(2)
-        tr("m", 1, 0, 6)
-        tr("m", 1, 1, 5)
-        co("m", 1, 0, S)
-        co("m", 1, 1, S)
-        q1("m", 1)
-        mn(2, (0,))
-        mn(2, (1,))
-        mn(2, (2,))
-        mn(2, (3,))
-        sq(3, (0,))
-        sq(3, (1,))
-        sq(3, (2,))
-        sq(3, (3,))
-        rn(3)
-        tr("m", 2, 0, 2)
-        tr("m", 2, 1, 3)
-        co("m", 2, 0, S)
-        co("m", 2, 1, S)
-        q1("m", 2)
-        mn(3, (0,))
-        mns(3, (1,))
-        mns(3, (2,))
-        mns(3, (3,))
-        tr("m", 3, 0, 6)
-        tr("m", 3, 1, 4)
-        co("m", 3, 0, S)
-        co("m", 3, 1, S)
-        q1("m", 3)
-        tr("k", 1, 0, 5)
-        tr("k", 1, 1, 7)
-        cl(0, 0)
-        rmax(0, 0)
-        cl(0, 1)
-        rmax(0, 1)
-        cl(0, 2)
-        rmax(0, 2)
-        cl(0, 3)
-        rmax(0, 3)
-        nm(0)
-        co("k", 1, 0, S)
-        co("k", 1, 1, S)
-        q1("k", 1)
-        prepg("er", 0, 0)
-        prepg("er", 0, 1)
-        prepg("er", 0, 2)
-        prepg("er", 0, 3)
-        prepq("er", 0)
-        ex1(0, 0)
-        ex1(0, 1)
-        ex1(0, 2)
-        ex1(0, 3)
-        cl(1, 0)
-        rmax(1, 0)
-        cl(1, 1)
-        rmax(1, 1)
-        cl(1, 2)
-        rmax(1, 2)
-        cl(1, 3)
-        rmax(1, 3)
-        nm(1)
-        ex1(1, 0)
-        ex1(1, 1)
-        ex1(1, 2)
-        ex1(1, 3)
-        prepg("ad", 0, 0)
-        prepg("ad", 0, 1)
-        prepg("ad", 0, 2)
-        prepg("ad", 0, 3)
-        prepq("ad", 0)
-        cl(2, 0)
-        rmax(2, 0)
-        cl(2, 1)
-        rmax(2, 1)
-        cl(2, 2)
-        rmax(2, 2)
-        cl(2, 3)
-        rmax(2, 3)
-        nm(2)
-        ex1(2, 0)
-        ex1(2, 1)
-        ex1(2, 2)
-        ex1(2, 3)
-        prepg("er", 1, 0)
-        prepg("er", 1, 1)
-        prepg("er", 1, 2)
-        prepg("er", 1, 3)
-        prepq("er", 1)
-        cl(3, 0)
-        rmax(3, 0)
-        cl(3, 1)
-        rmax(3, 1)
-        cl(3, 2)
-        rmax(3, 2)
-        cl(3, 3)
-        rmax(3, 3)
-        nm(3)
-        ex1(3, 0)
-        ex1(3, 1)
-        ex1(3, 2)
-        ex1(3, 3)
-        prepg("ad", 1, 0)
-        prepg("ad", 1, 1)
-        prepg("ad", 1, 2)
-        prepg("ad", 1, 3)
-        prepq("ad", 1)
-        cl(4, 0)
-        rmax(4, 0)
-        cl(4, 1)
-        rmax(4, 1)
-        cl(4, 2)
-        rmax(4, 2)
-        cl(4, 3)
-        rmax(4, 3)
-        nm(4)
-        ex1(4, 0)
-        ex1(4, 1)
-        ex1(4, 2)
-        ex1(4, 3)
-        cf1(0)
-        cf2(0)
-        cf3(0)
-        cl(5, 0)
-        rmax(5, 0)
-        cl(5, 1)
-        rmax(5, 1)
-        cl(5, 2)
-        rmax(5, 2)
-        cl(5, 3)
-        rmax(5, 3)
-        nm(5)
-        ex1(5, 0)
-        ex1(5, 1)
-        ex1(5, 2)
-        ex1(5, 3)
-        wscale1(0, 0, 0)
-        wscale1(0, 0, 1)
-        wscale1(0, 0, 2)
-        wscale1(0, 0, 3)
-        wil(0, 0)
-        wqz(0, 0)
-        cl(6, 0)
-        rmax(6, 0)
-        cl(6, 1)
-        rmax(6, 1)
-        cl(6, 2)
-        rmax(6, 2)
-        cl(6, 3)
-        rmax(6, 3)
-        nm(6)
-        ex1(6, 0)
-        ex1(6, 1)
-        ex1(6, 2)
-        ex1(6, 3)
-        wscale1(0, 1, 0)
-        wscale1(0, 1, 1)
-        wscale1(0, 1, 2)
-        wscale1(0, 1, 3)
-        wil(0, 1)
-        wqz(0, 1)
-        cl(7, 0)
-        rmax(7, 0)
-        cl(7, 1)
-        rmax(7, 1)
-        cl(7, 2)
-        rmax(7, 2)
-        cl(7, 3)
-        rmax(7, 3)
-        nm(7)
-        ex1(7, 0)
-        ex1(7, 1)
-        ex1(7, 2)
-        ex1(7, 3)
-        wil(0, 2)
-        wqz(0, 2)
-        wilg(0, 3, 0)
-        wilg(0, 3, 1)
-        wilg(0, 3, 2)
-        wilg(0, 3, 3)
-        wqz(0, 3)
-        cf1(1)
-        cf2(1)
-        cf3(1)
-        wil(1, 0)
-        wqz(1, 0)
-        wscale1(1, 1, 0)
-        wscale1(1, 1, 1)
-        wscale1(1, 1, 2)
-        wscale1(1, 1, 3)
-        wil(1, 1)
-        wqz(1, 1)
-        mm2("er", 0)
-        wscale1(1, 2, 0)
-        wscale1(1, 2, 1)
-        wscale1(1, 2, 2)
-        wscale1(1, 2, 3)
-        wil(1, 2)
-        wqz(1, 2)
-        mm2("er", 1)
-        mm2("ad", 0)
-        ea(0)
-        eo(0)
-        mm2("er", 2)
-        mm2("ad", 1)
-        ef(1)
-        em(1)
-        eo(1)
-        mm2("er", 3)
-        mm2("ad", 2)
-        ea(2)
-        eo(2)
-        mm2("er", 4)
-        mm2("ad", 3)
-        ef(3)
-        em(3)
-        eo(3)
-        oi(0, 0, 512, S)
-        oq(0, 0, 512)
-        wilg(1, 3, 0)
-        wilg(1, 3, 1)
-        wilg(1, 3, 2)
-        wilg(1, 3, 3)
-        wqz(1, 3)
-        mm2("er", 5)
-        mm2("ad", 4)
-        ea(4)
-        eo(4)
-        mm2("er", 6)
-        mm2("ad", 5)
-        ef(5)
-        em(5)
-        eo(5)
-        mm2("er", 7)
-        mm2("ad", 6)
-        ea(6)
-        eo(6)
-        mm2("er", 8)
-        mm2("ad", 7)
-        ef(7)
-        em(7)
-        eo(7)
-        oi(1, 0, 512, S)
-        oq(1, 0, 512)
-        mm2("er", 9)
-        mm2("ad", 8)
-        ea(8)
-        eo(8)
-        mm2("er", 10)
-        mm2("ad", 9)
-        ef(9)
-        em(9)
-        eo(9)
-        mm2("er", 11)
-        mm2("ad", 10)
-        ea(10)
-        eo(10)
-        mm2("er", 12)
-        mm2("ad", 11)
-        ef(11)
-        em(11)
-        eo(11)
-        oi(2, 0, 512, S)
-        oq(2, 0, 512)
-        mm2("er", 13)
-        mm2("ad", 12)
-        ea(12)
-        eo(12)
-        mm2("er", 14)
-        mm2("ad", 13)
-        ef(13)
-        em(13)
-        eo(13)
-        mm2("er", 15)
-        mm2("ad", 14)
-        ea(14)
-        eo(14)
-        mm2("ad", 15)
-        ef(15)
-        em(15)
-        eo(15)
-        oi(3, 0, 256, S)
-        oq(3, 0, 256)
-        oi(3, 256, 512, V)
-        oq(3, 256, 512)
+        every = range(J)
+        spread_gain()
+        for t in (0, 1):
+            square_on_scalar(0, t)
+        for g, t in ((0, 2), (0, 3), (1, 3), (2, 3)):
+            square_on_vector(g, t)
+        keep_gain()
+        inverse_length(0)
+        for h in range(2):
+            turn("key", 0, h, h)
+        for t in (1, 2, 3):
+            gain_on_gpsimd(3, t)
+        for t in every:
+            norm_on_vector(0, t)
+        turn("mem", 0, 0, 2)
+        turn("mem", 0, 1, 3)
+        rest = [(1, 0), (1, 1), (1, 2), (2, 0), (2, 1), (2, 2), (3, 0), (3, 1), (3, 2), (3, 3)]
+        for n, (g, t) in enumerate(rest):
+            square_on_scalar(g, t)
+            if n >= 2 and rest[n - 2][0] != rest[n - 1][0]:
+                inverse_length(rest[n - 2][0])
+        unload("key", 0, 0)
+        inverse_length(3)
+        for t in every:
+            norm_on_vector(1, t)
+        turn("mem", 1, 0, 6)
+        turn("mem", 1, 1, 5)
+        for t in every:
+            norm_on_vector(2, t)
+        norm_on_vector(3, 0)
+        unload("mem", 0, 0)
+        unload("mem", 0, 1)
+        unload("key", 0, 1)
+        quantize_rows("mem", 0)
+        quantize_rows("key", 0)
+        unload("mem", 1, 0)
+        unload("mem", 1, 1)
+        quantize_rows("mem", 1)
+        for t in (1, 2, 3):
+            norm_on_scalar(3, t)
+        turn("mem", 2, 0, 2)
+        turn("mem", 2, 1, 3)
+        interleave_write("erase", 0)
+        interleave_write("add", 0)
+        for c in (0, 1):
+            logits(0, c)
+        for c in (0, 1):
+            largest(0, c)
+        turn("mem", 3, 0, 6)
+        turn("mem", 3, 1, 4)
+        turn("key", 1, 0, 5)
+        turn("key", 1, 1, 7)
+        quantize_write("erase", 0)
+        for g in (2, 3):
+            for h in range(2):
+                unload("mem", g, h)
+            quantize_rows("mem", g)
+        for h in range(2):
+            unload("key", 1, h)
+        for c in (2, 3):
+            logits(0, c)
+        for c in (2, 3):
+            largest(0, c)
+
+        at_once = (3, 4, 6)
+        for i in range(1, TILES):
+            for c in range(NG):
+                logits(i, c)
+            for c in range(NG):
+                largest(i, c)
+                if c == 0 and i - 1 not in at_once:
+                    exponentials(i - 1)
+                if (i, c) == (5, 0):
+                    row_sums(0)
+                    quantize_write("erase", 1)
+                    invert_sums(0)
+                if (i, c) == (5, 1):
+                    row_factors(0)
+                if (i, c) == (6, 0):
+                    scale_rows(0, 1)
+            if i == 1:
+                interleave_write("erase", 1)
+                interleave_write("add", 1)
+            if i == 3:
+                quantize_rows("key", 1)
+                quantize_write("add", 0)
+            if i in at_once:
+                exponentials(i)
+            if i == 5:
+                scale_rows(0, 0)
+                for k in range(G // PIECE):
+                    scale_and_interleave_piece(0, 3, k)
+
+        interleave(0, 0)
+        exponentials(TILES - 1)
+        interleave(0, 1)
+        quantize_w(0, 0)
+        quantize_w(0, 1)
+        scale_and_interleave(0, 2)
+        row_sums(1)
+        quantize_w(0, 3)
+        invert_sums(1)
+        quantize_w(0, 2)
+        row_factors(1)
+        quantize_write("add", 1)
+        scale_rows(1, 1)
+        scale_rows(1, 2)
+        scale_and_interleave_piece(1, 3, 0)
+        scale_and_interleave(1, 0)
+        interleave(1, 1)
+        quantize_w(1, 0)
+        quantize_w(1, 1)
+        interleave(1, 2)
+
+        vector_after = {
+            0: [(keep_on_vector, 2)],
+            2: [(keep_on_vector, 4), (quantize_w, 1, 2)],
+            4: [(keep_on_vector, 6), (keep_on_vector, 8)],
+            6: [(keep_on_vector, 10)],
+            7: [(quantize_result, 0, 0), (quantize_w, 1, 3)],
+            8: [(keep_on_vector, 12), (quantize_result, 0, 1), (store_planes, 0)],
+            10: [(quantize_result, 1, 0)],
+            12: [(quantize_result, 1, 1), (store_planes, 1), (keep_on_vector, 14), (quantize_result, 2, 0)],
+            14: [(quantize_result, 2, 1), (store_planes, 2)],
+        }
+        scalar_after = {
+            7: [(round_on_scalar, 0, 0), (round_on_scalar, 0, 1)],
+            9: [(round_on_scalar, 1, 0)],
+            13: [(round_on_scalar, 1, 1), (round_on_scalar, 2, 0)],
+            15: [(round_on_scalar, 2, 1)],
+        }
+        gpsimd_after = {
+            3: [(scale_and_interleave_piece, 1, 3, 1)],
+            7: [(scale_and_interleave_piece, 1, 3, 2), (scale_and_interleave_piece, 1, 3, 3)],
+        }
+        for j in range(3):
+            product("erase", j)
+        product("add", 0)
+        product("erase", 3)
+        product("add", 1)
+        keep_on_vector(0)
+        left_on_scalar(1)
+        keep_on_gpsimd(1)
+        last = NG * J - 1
+        for j in range(NG * J):
+            if j + 4 <= last:
+                product("erase", j + 4)
+            if j + 2 <= last:
+                product("add", j + 2)
+            finish(j)
+            for call in vector_after.get(j, []):
+                call[0](*call[1:])
+            if j % 2 == 1 and j + 2 <= last:
+                left_on_scalar(j + 2)
+                keep_on_gpsimd(j + 2)
+                for call in scalar_after.get(j + 2, []) + gpsimd_after.get(j + 2, []):
+                    call[0](*call[1:])
+        round_on_scalar(NG - 1, 0)
+        round_on_vector(NG - 1, 1)
+        quantize_result(NG - 1, 1)
+        quantize_result(NG - 1, 0)
+        store_planes(NG - 1)

from contextlib import ExitStack

import concourse.mybir as mybir
from concourse.masks import make_identity

T, N, W = 1024, 2048, 512
P = 128
J = 4
G = P * J
TG, NG = T // G, N // G
TILES = TG * J
HALF = W // 2
RUN = 4
PIECE = 128
FLOPS = 3 * 2 * T * N * W

F32 = mybir.dt.float32
BF16 = mybir.dt.bfloat16
U32 = mybir.dt.uint32
I32 = mybir.dt.int32
U8 = mybir.dt.uint8
FP8X4 = mybir.dt.float8_e4m3fn_x4
ALU = mybir.AluOpType
ACT = mybir.ActivationFunctionType
X = mybir.AxisListType.X


def row_tiles(x, g):
    return x.rearrange("(g p t) w -> g p t w", p=P, t=J)[g]


def by_runs(x):
    return x.rearrange("p t (c i) -> p c t i", i=RUN)


def into_words(x):
    return x.rearrange("p (c i) t -> p c t i", i=RUN)


def tile_ntmcontentaddresseraseadd_x1_kernel(tc, key, mem, gm, s, erase, add, out_0, out_1, out_2):
    nc = tc.nc
    with ExitStack() as ctx:
        keep = ctx.enter_context(tc.tile_pool(name="keep", bufs=1))
        work = ctx.enter_context(tc.tile_pool(name="work", bufs=2))
        psum = ctx.enter_context(tc.psum_pool(name="psum", bufs=1))
        ctx.enter_context(tc.manual_schedule())

        def kept(name, shape, dtype):
            return keep.tile(shape, dtype, name=name, tag=name, align_bytes=64)

        def passing(name, shape, dtype, bufs):
            return work.tile(shape, dtype, name=name, tag=name, bufs=bufs, align_bytes=64)

        def bank(k, name):
            return psum.tile([P, 512], F32, name=name, tag="bank%d" % k)

        mem_rows = [kept("mem%d" % g, [P, J, W], BF16) for g in range(NG)]
        key_rows = [kept("key%d" % g, [P, J, W], BF16) for g in range(TG)]
        write_keys = [(what, g) for g in range(TG) for what in ("erase", "add")]
        write_rows = {k: kept("%s%d" % k, [P, J, W], BF16) for k in write_keys}
        gain_row = kept("gain_row", [P, W], BF16)
        gain = kept("gain", [P, W], F32)
        ones_in = kept("ones_in", [P, P], BF16)
        ones = kept("ones", [P, P], BF16)
        identity = kept("identity", [P, P], F32)
        strength = kept("strength", [P, TG, J], BF16)
        squares = kept("squares", [P, NG, J], F32)
        inverse = kept("inverse", [P, NG, J], F32)
        row_max = kept("row_max", [P, TILES, NG], F32)
        minus_max = kept("minus_max", [P, TILES], F32)
        sums = kept("sums", [P, TILES, NG], F32)
        total = kept("total", [P, TG, J], F32)
        inverse_total = kept("inverse_total", [P, TG, J], F32)
        factor = kept("factor", [P, TG, J], F32)

        mem_q = kept("mem_q", [P, NG, G], U32), kept("mem_s", [P, NG, G], U8)
        key_q = kept("key_q", [P, TG, G], U32), kept("key_s", [P, TG, G], U8)
        w_q = [kept("w_q%d" % g, [P, N], U32) for g in range(TG)]
        w_s = [kept("w_s%d" % g, [P, N], U8) for g in range(TG)]
        write_q = {k: kept("%s_q%d" % k, [P, W], U32) for k in write_keys}
        write_s = {k: kept("%s_s%d" % k, [P, W], U8) for k in write_keys}
        exps = [kept("exps0", [P, J, N], F32), kept("exps1", [P, J, N], F32)]

        nc.vector.memset(gain_row[:], 0.0)
        nc.vector.memset(ones_in[:], 1.0)
        make_identity(nc, identity[:])
        nc.sync.dma_start(out=mem_rows[0][:, 0:2, :], in_=row_tiles(mem, 0)[:, 0:2, :])
        nc.sync.dma_start(out=gain_row[0:1, :], in_=gm.rearrange("(o w) -> o w", o=1))
        nc.sync.dma_start(out=mem_rows[0][:, 2:4, :], in_=row_tiles(mem, 0)[:, 2:4, :])
        nc.sync.dma_start(out=key_rows[0][:], in_=row_tiles(key, 0))
        for g in range(1, NG):
            nc.sync.dma_start(out=mem_rows[g][:], in_=row_tiles(mem, g))
        nc.sync.dma_start(out=key_rows[1][:], in_=row_tiles(key, 1))
        nc.sync.dma_start(out=strength[:], in_=s.rearrange("(g p t) -> p g t", p=P, t=J))
        for g in range(TG):
            nc.sync.dma_start(out=write_rows["erase", g][:], in_=row_tiles(erase, g))
            nc.sync.dma_start(out=write_rows["add", g][:], in_=row_tiles(add, g))
        nc.scalar.activation(out=ones[:], in_=ones_in[:], func=ACT.Abs_reciprocal_sqrt)

        gain_bank, scaled_rows, normed, turned, words, logit_bank = {}, {}, {}, {}, {}, {}
        writes, w_rows, w_words, product_bank, kept_part, left_factor = {}, {}, {}, {}, {}, {}
        result, result_words, planes = {}, {}, {}

        def spread_gain():
            gain_bank[0] = bank(7, "gain_bank")
            nc.tensor.matmul(gain_bank[0][:], lhsT=ones[:], rhs=gain_row[:], start=True, stop=True)

        def keep_gain():
            nc.scalar.copy(gain[:], gain_bank[0][:])

        def square_on_scalar(g, t):
            unused = passing("squared_s", [P, W], BF16, 2)
            nc.scalar.activation(
                out=unused[:], in_=mem_rows[g][:, t, :], func=ACT.Square, accum_out=squares[:, g, t : t + 1]
            )

        def square_on_vector(g, t):
            unused = passing("squared_v", [P, W], BF16, 2)
            x = mem_rows[g][:, t, :]
            nc.vector.scalar_tensor_tensor(
                out=unused[:], in0=x, scalar=1.0, in1=x, op0=ALU.mult, op1=ALU.mult, accum_out=squares[:, g, t : t + 1]
            )

        def inverse_length(g):
            nc.scalar.activation(out=inverse[:, g, :], in_=squares[:, g, :], func=ACT.Abs_reciprocal_sqrt, bias=1e-6)

        def norm_on_vector(g, t):
            normed[g, t] = passing("normed_v", [P, W], BF16, 4)
            nc.vector.scalar_tensor_tensor(
                out=normed[g, t][:],
                in0=mem_rows[g][:, t, :],
                scalar=inverse[:, g, t : t + 1],
                in1=gain_bank[0][:],
                op0=ALU.mult,
                op1=ALU.mult,
            )

        def gain_on_gpsimd(g, t):
            scaled_rows[g, t] = passing("scaled_row", [P, W], F32, 4)
            nc.gpsimd.tensor_tensor(out=scaled_rows[g, t][:], in0=mem_rows[g][:, t, :], in1=gain[:], op=ALU.mult)

        def norm_on_scalar(g, t):
            normed[g, t] = passing("normed_s", [P, W], BF16, 3)
            nc.scalar.activation(
                out=normed[g, t][:], in_=scaled_rows[g, t][:], func=ACT.Copy, scale=inverse[:, g, t : t + 1]
            )

        def turn(what, g, h, k):
            turned[what, g, h] = bank(k, "turned")
            view = turned[what, g, h][:].rearrange("p (i u r) -> p i u r", i=2, u=2)
            for i in range(2):
                t = 2 * h + i
                rows = key_rows[g][:, t, :] if what == "key" else normed[g, t][:]
                for u in range(2):
                    nc.tensor.transpose(view[:, i, u, :], rows.bitcast(F32)[:, u::2], identity[:])

        def unload(what, g, h):
            if h == 0:
                words[what, g] = passing("words", [P, G, J], BF16, 3)
            pairs = words[what, g][:].rearrange("p n j -> p (n j)").bitcast(F32)[:, h * 512 : (h + 1) * 512]
            nc.scalar.copy(
                pairs.rearrange("p (i r u) -> p i r u", i=2, u=2),
                turned[what, g, h][:].rearrange("p (i u r) -> p i r u", i=2, u=2),
            )

        def quantize_rows(what, g):
            codes, scales = key_q if what == "key" else mem_q
            nc.vector.quantize_mx(
                out=codes[:, g, :].bitcast(FP8X4),
                scales=scales[:, g, :],
                in_=words[what, g][:].rearrange("p n j -> p (n j)"),
            )

        def logits(i, c):
            tg, t = divmod(i, J)
            cols = slice(t * P, (t + 1) * P)
            logit_bank[i, c] = bank(i % 2 * NG + c, "logits")
            nc.tensor.matmul_mx(
                out=logit_bank[i, c][:],
                lhsT=key_q[0][:, tg, cols].bitcast(FP8X4),
                lhsT_scale=key_q[1][:, tg, cols],
                rhs=mem_q[0][:, c, :].bitcast(FP8X4),
                rhs_scale=mem_q[1][:, c, :],
                start=True,
                stop=True,
            )

        def largest(i, c):
            nc.vector.tensor_reduce(out=row_max[:, i, c : c + 1], in_=logit_bank[i, c][:], axis=X, op=ALU.max)

        def exponentials(i):
            tg, t = divmod(i, J)
            nc.vector.tensor_reduce(out=minus_max[:, i : i + 1], in_=row_max[:, i, :], axis=X, op=ALU.max, negate=True)
            for c in range(NG):
                nc.scalar.activation(
                    out=exps[tg][:, t, c * G : (c + 1) * G],
                    in_=logit_bank[i, c][:],
                    func=ACT.Exp,
                    bias=minus_max[:, i : i + 1],
                    accum_out=sums[:, i, c : c + 1],
                )

        def row_sums(tg):
            nc.vector.tensor_reduce(out=total[:, tg, :], in_=sums[:, tg * J : (tg + 1) * J, :], axis=X, op=ALU.add)

        def invert_sums(tg):
            nc.vector.reciprocal(inverse_total[:, tg, :], total[:, tg, :])

        def row_factors(tg):
            nc.vector.scalar_tensor_tensor(
                out=factor[:, tg, :],
                in0=strength[:, tg, :],
                scalar=64.0,
                in1=inverse_total[:, tg, :],
                op0=ALU.mult,
                op1=ALU.mult,
            )

        def scale_rows(tg, c):
            w_rows[tg, c] = passing("w_rows", [P, J, G], BF16, 2)
            for t in range(J):
                nc.scalar.activation(
                    out=w_rows[tg, c][:, t, :],
                    in_=exps[tg][:, t, c * G : (c + 1) * G],
                    func=ACT.Copy,
                    scale=factor[:, tg, t : t + 1],
                )

        def interleave(tg, c):
            w_words[tg, c] = passing("w_words", [P, G, J], BF16, 2)
            nc.vector.tensor_copy(out=into_words(w_words[tg, c][:]), in_=by_runs(w_rows[tg, c][:]))

        def scale_and_interleave(tg, c):
            w_words[tg, c] = passing("w_words", [P, G, J], BF16, 2)
            nc.vector.tensor_tensor(
                out=w_words[tg, c][:],
                in0=exps[tg][:, :, c * G : (c + 1) * G].rearrange("p t n -> p n t"),
                in1=factor[:, tg, :].unsqueeze(1).to_broadcast([P, G, J]),
                op=ALU.mult,
            )

        def scale_and_interleave_piece(tg, c, k):
            if k == 0:
                w_words[tg, c] = passing("w_words_g", [P, G, J], BF16, 1)
            cols = slice(k * PIECE, (k + 1) * PIECE)
            from_cols = slice(c * G + k * PIECE, c * G + (k + 1) * PIECE)
            nc.gpsimd.tensor_tensor(
                out=w_words[tg, c][:, cols, :],
                in0=exps[tg][:, :, from_cols].rearrange("p t n -> p n t"),
                in1=factor[:, tg, :].unsqueeze(1).to_broadcast([P, PIECE, J]),
                op=ALU.mult,
            )

        def quantize_w(tg, c):
            cols = slice(c * G, (c + 1) * G)
            nc.vector.quantize_mx(
                out=w_q[tg][:, cols].bitcast(FP8X4),
                scales=w_s[tg][:, cols],
                in_=w_words[tg, c][:].rearrange("p n t -> p (n t)"),
            )

        def interleave_write(what, g):
            writes[what, g] = passing("write_words", [P, W, J], BF16, 2)
            for k in range(W // PIECE):
                cols = slice(k * PIECE, (k + 1) * PIECE)
                nc.gpsimd.tensor_scalar(
                    out=writes[what, g][:, cols, :],
                    in0=write_rows[what, g][:, :, cols].rearrange("p t w -> p w t"),
                    scalar1=1.0,
                    scalar2=0.0,
                    op0=ALU.mult,
                    op1=ALU.add,
                )

        def quantize_write(what, g):
            nc.vector.quantize_mx(
                out=write_q[what, g][:].bitcast(FP8X4),
                scales=write_s[what, g][:],
                in_=writes[what, g][:].rearrange("p w t -> p (w t)"),
            )

        def product(what, j):
            cols = slice(j * P, (j + 1) * P)
            product_bank[what, j] = bank((2 * j + (7 if what == "erase" else 2)) % 8, what)
            for tg in range(TG):
                nc.tensor.matmul_mx(
                    out=product_bank[what, j][:],
                    lhsT=w_q[tg][:, cols].bitcast(FP8X4),
                    lhsT_scale=w_s[tg][:, cols],
                    rhs=write_q[what, tg][:].bitcast(FP8X4),
                    rhs_scale=write_s[what, tg][:],
                    start=(tg == 0),
                    stop=(tg == TG - 1),
                )

        def keep_on_vector(j):
            g, t = divmod(j, J)
            kept_part[j] = passing("kept_v", [P, W], F32, 3), ALU.subtract
            nc.vector.scalar_tensor_tensor(
                out=kept_part[j][0][:],
                in0=product_bank["erase", j][:],
                scalar=1.0,
                in1=mem_rows[g][:, t, :],
                op0=ALU.subtract,
                op1=ALU.mult,
            )

        def left_on_scalar(j):
            left_factor[j] = passing("left_factor", [P, W], F32, 2)
            nc.scalar.activation(
                out=left_factor[j][:], in_=product_bank["erase", j][:], func=ACT.Copy, scale=-1.0, bias=1.0
            )

        def keep_on_gpsimd(j):
            g, t = divmod(j, J)
            kept_part[j] = passing("kept_g", [P, W], F32, 2), ALU.add
            nc.gpsimd.tensor_tensor(
                out=kept_part[j][0][:], in0=left_factor[j][:], in1=mem_rows[g][:, t, :], op=ALU.mult
            )

        def finish(j):
            g, t = divmod(j, J)
            if j == 0:
                space = keep.tile([P, NG, J, W], F32, name="result", tag="exps0", align_bytes=64)
                for n in range(NG):
                    result[n] = space[:, n, :, :]
            part, op = kept_part[j]
            nc.vector.tensor_tensor(out=result[g][:, t, :], in0=product_bank["add", j][:], in1=part[:], op=op)
            if t % 2 == 1:
                nc.sync.dma_start(out=row_tiles(out_0, g)[:, t - 1 : t + 1, :], in_=result[g][:, t - 1 : t + 1, :])

        def round_on_scalar(g, h):
            result_words[g, h] = passing("result_s", [P, HALF, J], BF16, 2)
            nc.scalar.copy(
                into_words(result_words[g, h][:]), by_runs(result[g][:, :, h * HALF : (h + 1) * HALF])
            )

        def round_on_vector(g, h):
            result_words[g, h] = passing("result_v", [P, HALF, J], BF16, 1)
            nc.vector.tensor_copy(
                out=into_words(result_words[g, h][:]), in_=by_runs(result[g][:, :, h * HALF : (h + 1) * HALF])
            )

        def quantize_result(g, h):
            if g not in planes:
                planes[g] = passing("out_q", [P, W], U32, 2), passing("out_s", [P, W], U8, 2)
            codes, scales = planes[g]
            cols = slice(h * HALF, (h + 1) * HALF)
            nc.vector.quantize_mx(
                out=codes[:, cols].bitcast(FP8X4),
                scales=scales[:, cols],
                in_=result_words[g, h][:].rearrange("p w t -> p (w t)"),
            )

        def store_planes(g):
            codes, scales = planes[g]
            nc.sync.dma_start(out=out_1[g].rearrange("p m t -> p (m t)").bitcast(I32), in_=codes[:].bitcast(I32))
            for q in range(4):
                nc.sync.dma_start(
                    out=out_2[g, 4 * q : 4 * q + 4, :].bitcast(I32), in_=scales[32 * q : 32 * q + 4, :].bitcast(I32)
                )

        every = range(J)
        spread_gain()
        for t in (0, 1):
            square_on_scalar(0, t)
        for g, t in ((0, 2), (0, 3), (1, 3), (2, 3)):
            square_on_vector(g, t)
        keep_gain()
        inverse_length(0)
        for h in range(2):
            turn("key", 0, h, h)
        for t in (1, 2, 3):
            gain_on_gpsimd(3, t)
        for t in every:
            norm_on_vector(0, t)
        turn("mem", 0, 0, 2)
        turn("mem", 0, 1, 3)
        rest = [(1, 0), (1, 1), (1, 2), (2, 0), (2, 1), (2, 2), (3, 0), (3, 1), (3, 2), (3, 3)]
        for n, (g, t) in enumerate(rest):
            square_on_scalar(g, t)
            if n >= 2 and rest[n - 2][0] != rest[n - 1][0]:
                inverse_length(rest[n - 2][0])
        unload("key", 0, 0)
        inverse_length(3)
        for t in every:
            norm_on_vector(1, t)
        turn("mem", 1, 0, 6)
        turn("mem", 1, 1, 5)
        for t in every:
            norm_on_vector(2, t)
        norm_on_vector(3, 0)
        unload("mem", 0, 0)
        unload("mem", 0, 1)
        unload("key", 0, 1)
        quantize_rows("mem", 0)
        quantize_rows("key", 0)
        unload("mem", 1, 0)
        unload("mem", 1, 1)
        quantize_rows("mem", 1)
        for t in (1, 2, 3):
            norm_on_scalar(3, t)
        turn("mem", 2, 0, 2)
        turn("mem", 2, 1, 3)
        interleave_write("erase", 0)
        interleave_write("add", 0)
        for c in (0, 1):
            logits(0, c)
        for c in (0, 1):
            largest(0, c)
        turn("mem", 3, 0, 6)
        turn("mem", 3, 1, 4)
        turn("key", 1, 0, 5)
        turn("key", 1, 1, 7)
        quantize_write("erase", 0)
        for g in (2, 3):
            for h in range(2):
                unload("mem", g, h)
            quantize_rows("mem", g)
        for h in range(2):
            unload("key", 1, h)
        for c in (2, 3):
            logits(0, c)
        for c in (2, 3):
            largest(0, c)

        at_once = (3, 4, 6)
        for i in range(1, TILES):
            for c in range(NG):
                logits(i, c)
            for c in range(NG):
                largest(i, c)
                if c == 0 and i - 1 not in at_once:
                    exponentials(i - 1)
                if (i, c) == (5, 0):
                    row_sums(0)
                    quantize_write("erase", 1)
                    invert_sums(0)
                if (i, c) == (5, 1):
                    row_factors(0)
                if (i, c) == (6, 0):
                    scale_rows(0, 1)
            if i == 1:
                interleave_write("erase", 1)
                interleave_write("add", 1)
            if i == 3:
                quantize_rows("key", 1)
                quantize_write("add", 0)
            if i in at_once:
                exponentials(i)
            if i == 5:
                scale_rows(0, 0)
                for k in range(G // PIECE):
                    scale_and_interleave_piece(0, 3, k)

        interleave(0, 0)
        exponentials(TILES - 1)
        interleave(0, 1)
        quantize_w(0, 0)
        quantize_w(0, 1)
        scale_and_interleave(0, 2)
        row_sums(1)
        quantize_w(0, 3)
        invert_sums(1)
        quantize_w(0, 2)
        row_factors(1)
        quantize_write("add", 1)
        scale_rows(1, 1)
        scale_rows(1, 2)
        scale_and_interleave_piece(1, 3, 0)
        scale_and_interleave(1, 0)
        interleave(1, 1)
        quantize_w(1, 0)
        quantize_w(1, 1)
        interleave(1, 2)

        vector_after = {
            0: [(keep_on_vector, 2)],
            2: [(keep_on_vector, 4), (quantize_w, 1, 2)],
            4: [(keep_on_vector, 6), (keep_on_vector, 8)],
            6: [(keep_on_vector, 10)],
            7: [(quantize_result, 0, 0), (quantize_w, 1, 3)],
            8: [(keep_on_vector, 12), (quantize_result, 0, 1), (store_planes, 0)],
            10: [(quantize_result, 1, 0)],
            12: [(quantize_result, 1, 1), (store_planes, 1), (keep_on_vector, 14), (quantize_result, 2, 0)],
            14: [(quantize_result, 2, 1), (store_planes, 2)],
        }
        scalar_after = {
            7: [(round_on_scalar, 0, 0), (round_on_scalar, 0, 1)],
            9: [(round_on_scalar, 1, 0)],
            13: [(round_on_scalar, 1, 1), (round_on_scalar, 2, 0)],
            15: [(round_on_scalar, 2, 1)],
        }
        gpsimd_after = {
            3: [(scale_and_interleave_piece, 1, 3, 1)],
            7: [(scale_and_interleave_piece, 1, 3, 2), (scale_and_interleave_piece, 1, 3, 3)],
        }
        for j in range(3):
            product("erase", j)
        product("add", 0)
        product("erase", 3)
        product("add", 1)
        keep_on_vector(0)
        left_on_scalar(1)
        keep_on_gpsimd(1)
        last = NG * J - 1
        for j in range(NG * J):
            if j + 4 <= last:
                product("erase", j + 4)
            if j + 2 <= last:
                product("add", j + 2)
            finish(j)
            for call in vector_after.get(j, []):
                call[0](*call[1:])
            if j % 2 == 1 and j + 2 <= last:
                left_on_scalar(j + 2)
                keep_on_gpsimd(j + 2)
                for call in scalar_after.get(j + 2, []) + gpsimd_after.get(j + 2, []):
                    call[0](*call[1:])
        round_on_scalar(NG - 1, 0)
        round_on_vector(NG - 1, 1)
        quantize_result(NG - 1, 1)
        quantize_result(NG - 1, 0)
        store_planes(NG - 1)
